import numpy as np
CORES = [24,48,72,152,176,200]
N = 6
TK = 256
D = 128 * N
EPS = 0.01
def setup_inputs(rng):
    x = rng.standard_normal((N, 128, TK), dtype=np.float32) * (0.5 + np.abs(rng.standard_normal((1, 1, TK), dtype=np.float32))) + rng.standard_normal((1, 1, TK), dtype=np.float32)
    return {"x": x, "dy": rng.standard_normal((N, 128, TK), dtype=np.float32) + 0.5 * x + rng.standard_normal((1, 1, TK), dtype=np.float32)}
def setup_inputs_big(rng):
    d = setup_inputs(rng)
    for k in ("x", "dy"): d[k] = (d[k].astype(np.float32) * 1024.0).astype(d[k].dtype)
    return d
def setup_inputs_small(rng):
    d = setup_inputs(rng)
    for k in ("x", "dy"): d[k] = (d[k].astype(np.float32) * (1 / 1024.0)).astype(d[k].dtype)
    return d
def setup_inputs_apart(rng):
    d = setup_inputs(rng)
    f = (10.0 ** rng.permutation(np.linspace(-1.5, 1.5, N))).astype(np.float32).reshape(N, 1, 1)
    for k in ("x",): d[k] = (d[k].astype(np.float32) * f).astype(d[k].dtype)
    return d
def setup_inputs_mixed(rng):
    d = setup_inputs(rng)
    f = (10.0 ** rng.uniform(-3, 3, (1, 1, TK))).astype(np.float32); shape = rng.integers(3, size=(1, 1, TK))
    for k in ("x", "dy"):
        x = d[k].astype(np.float32)
        m = x.mean(axis=(0, 1), keepdims=True); level = m + np.sign(x - m) * np.abs(x - m).mean(axis=(0, 1), keepdims=True) * rng.uniform(0.9, 1.1, x.shape).astype(np.float32)
        other = x * np.where(rng.random(x.shape) < 0.5, 0.1, 1.0).astype(np.float32)
        d[k] = (np.where(shape == 1, level, np.where(shape == 2, other, x)) * f).astype(d[k].dtype)
    return d
def setup_inputs_offset(rng):
    d = setup_inputs(rng)
    x = d["x"]; spread = x.std(axis=(0, 1), keepdims=True)
    d["x"] = (x + spread * rng.uniform(16, 48, (1, 1, TK)) * rng.choice([-1.0, 1.0], (1, 1, TK))).astype(np.float32)
    return d
def reference(x, dy):
    X, DY = x.astype(np.float64), dy.astype(np.float64)
    mu = X.sum(axis=(0, 1)) / D
    rs = 1.0 / np.sqrt(((X - mu) ** 2).sum(axis=(0, 1)) / D + EPS)
    n = (X - mu) * rs
    a = DY.sum(axis=(0, 1)) / D; c = (DY * n).sum(axis=(0, 1)) / D
    return {"dx": (rs * (DY - a - n * c)).astype(np.float32)}

@@ -1,0 +1,269 @@
+from concourse.bass import DstId, RemoteDMATransfer
+from concourse.mybir import AluOpType, AxisListType, ActivationFunctionType
+
+NSIM = 256
+NR = 6
+EPS = 0.01
+NSEM = 72
+
+SCRATCH = {
+    "xs": ("sbuf", [128, 256], "float32"),
+    "dys": ("sbuf", [128, 256], "float32"),
+    "ones": ("sbuf", [128, 128], "float32"),
+    "ident": ("sbuf", [128, 128], "float32"),
+    "land": ("sbuf", [128, NR, 4, 2], "float32"),
+    "xcs": ("sbuf", [128, 256], "float32"),
+    "pr": ("sbuf", [128, 256], "float32"),
+    "j1": ("sbuf", [128, 256], "float32"),
+    "j2": ("sbuf", [128, 256], "float32"),
+    "j3": ("sbuf", [128, 256], "float32"),
+    "jq": ("sbuf", [128, 16], "float32"),
+    "cn": ("sbuf", [128, 2], "float32"),
+    "a6": ("sbuf", [128, 2], "float32"),
+    "ia6": ("sbuf", [128, 2], "float32"),
+    "y0": ("sbuf", [128, 2], "float32"),
+    "y2": ("sbuf", [128, 2], "float32"),
+    "ye": ("sbuf", [128, 2], "float32"),
+    "yf": ("sbuf", [128, 2], "float32"),
+    "rsa": ("sbuf", [128, 2], "float32"),
+    "ida": ("sbuf", [128, 256], "float32"),
+    "t3": ("sbuf", [128, 3, 4, 2], "float32"),
+    "t1": ("sbuf", [128, 4, 2], "float32"),
+    "tot": ("sbuf", [128, 4, 2], "float32"),
+    "nmu": ("sbuf", [128, 2], "float32"),
+    "qm": ("sbuf", [128, 2], "float32"),
+    "tt": ("sbuf", [128, 2], "float32"),
+    "ct": ("sbuf", [128, 2], "float32"),
+    "nega": ("sbuf", [128, 2], "float32"),
+    "sdd": ("sbuf", [128, 2], "float32"),
+    "v6": ("sbuf", [128, 2], "float32"),
+    "iv6": ("sbuf", [128, 2], "float32"),
+    "bb": ("sbuf", [128, 2], "float32"),
+    "r1": ("sbuf", [128, 2], "float32"),
+    "dg": ("sbuf", [128, 256], "float32"),
+    "uu": ("sbuf", [128, 256], "float32"),
+    "vv": ("sbuf", [128, 256], "float32"),
+    "outs": ("sbuf", [128, 256], "float32"),
+    "px0": ("psum", [128, 512], "float32"),
+    "px1": ("psum", [128, 512], "float32"),
+    "pd0": ("psum", [128, 512], "float32"),
+    "pd1": ("psum", [128, 512], "float32"),
+    "po0": ("psum", [128, 512], "float32"),
+    "po1": ("psum", [128, 512], "float32"),
+}
+SEMAPHORES = ["arr", "sent"] + ["s%d" % i for i in range(NSEM)]
+
+
+def _bits(mask):
+    return bin(mask).count("1")
+
+
+def _plan(c, T, topo):
+    others = [p for p in T.cores if p != c]
+    direct = [p for p in others if topo.may_write(c, p)]
+    cross = [p for p in others if not topo.may_write(c, p)]
+    cand = [k for k in range(NSIM)
+            if k != c and T.rank_of(k) is None and topo.host(k) == topo.host(c) and topo.chip(k) == topo.chip(c)
+            and all(topo.may_write(k, p) for p in cross)]
+    cand.sort(key=lambda k: (topo.die(k) != topo.die(c), k))
+    relay = [(cand[i // 2], cross[i:i + 2]) for i in range(0, len(cross), 2)]
+    return direct, relay
+
+
+def _chip_mask(c, direct, relay, topo):
+    m = topo.mask(c, relay[0][0])
+    for p in direct:
+        if m & ~topo.mask(c, p):
+            m = m & ~topo.mask(c, p)
+    return m
+
+
+def _send(g, core, T, topo, r, dests, mask):
+    ids = []
+    for d in dests:
+        rid, pid = topo.addr(d, core)
+        ids.append(DstId(rid=rid, pnc=pid))
+    g.remote_dma_fused(
+        [RemoteDMATransfer(dst_ids=ids, dma_engine_mask=mask, remote_sem=T.sem.arr,
+                           srcs=[T.land[:, r]], dsts=[T.land[:, r] for d in dests], alu_op=0)],
+        local_sem=T.sem.sent)
+    return _bits(mask)
+
+
+def rank_program(g, core, T, topo):
+    rank = T.rank_of(core)
+    if rank is None:
+        for r, c in enumerate(T.cores):
+            direct, relay = _plan(c, T, topo)
+            for h, dests in relay:
+                if h == core:
+                    g.wait_ge(T.sem.arr, _bits(_chip_mask(c, direct, relay, topo)))
+                    n = _send(g, core, T, topo, r, dests, topo.mask(core, dests[0]))
+                    g.wait_ge(T.sem.sent, n)
+        return
+
+    V, A, P = g.vector, g.scalar, g.tensor
+    ALU, ACT = AluOpType, ActivationFunctionType
+    cnt = [0]
+    seen = {}
+
+    def sem():
+        i = cnt[0]
+        cnt[0] += 1
+        return i, T.sem["s%d" % i]
+
+    def done(instr):
+        i, s = sem()
+        instr.then_inc(s, 1)
+        return (i, s, 1)
+
+    def after(q, qn, toks):
+        for (i, s, v) in toks:
+            if (qn, i) not in seen:
+                seen[(qn, i)] = True
+                q.wait_ge(s, v)
+
+    def col(t, h):
+        return t[:, h:h + 1]
+
+    def st(k, h):
+        return T.land[:, rank, k, h:h + 1]
+
+    H = (slice(0, 128), slice(128, 256))
+    px = (T.px0[:, 0:128], T.px1[:, 0:128])
+    pd = (T.pd0[:, 0:128], T.pd1[:, 0:128])
+    po = (T.po0[:, 0:128], T.po1[:, 0:128])
+
+    ix, sx = sem()
+    idy, sdy = sem()
+    g.sync.dma_start(T.xs[0:64, :], T.x[0:64, :]).then_inc(sx, 16)
+    A.dma_start(T.xs[64:128, :], T.x[64:128, :]).then_inc(sx, 16)
+    g.sync.dma_start(T.dys[0:64, :], T.dy[0:64, :]).then_inc(sdy, 16)
+    A.dma_start(T.dys[64:128, :], T.dy[64:128, :]).then_inc(sdy, 16)
+    t_x, t_dy = (ix, sx, 32), (idy, sdy, 32)
+
+    t_ones = done(V.memset(T.ones[:], 1.0))
+    after(g, "g", [t_ones])
+    t_id = done(g.affine_select(T.ident[:], T.ones[:], [[-1, 128]], ALU.is_equal, 0.0, 0, 1))
+
+    after(P, "p", [t_id, t_x])
+    t_tx = [done(P.transpose(px[h], T.xs[:, H[h]], T.ident[:])) for h in (0, 1)]
+    after(P, "p", [t_dy])
+    t_td = [done(P.transpose(pd[h], T.dys[:, H[h]], T.ident[:])) for h in (0, 1)]
+
+    t_m, t_xc, t_m2 = [], [], []
+    for h in (0, 1):
+        after(A, "a", [t_tx[h]])
+        t_m.append(done(A.activation(T.j1[:, H[h]], px[h], ACT.Copy, scale=1.0 / 128, accum_out=st(0, h))))
+        after(V, "v", [t_m[h], t_tx[h]])
+        t_xc.append(done(V.tensor_scalar(out=T.xcs[:, H[h]], in0=px[h], scalar1=st(0, h), scalar2=-1.0 / 128,
+                                         op0=ALU.subtract, op1=ALU.mult)))
+        after(A, "a", [t_xc[h]])
+        t_m2.append(done(A.activation(T.j2[:, H[h]], T.xcs[:, H[h]], ACT.Square, scale=128.0, accum_out=st(2, h))))
+    t_s, t_c = [], []
+    for h in (0, 1):
+        after(V, "v", [t_td[h], t_xc[h]])
+        t_pr = done(V.tensor_tensor(out=T.pr[:, H[h]], in0=pd[h], in1=T.xcs[:, H[h]], op=ALU.mult))
+        after(A, "a", [t_pr, t_td[h]])
+        t_s.append(done(A.activation(T.j3[:, H[h]], pd[h], ACT.Copy, scale=-1.0 / 128, accum_out=st(1, h))))
+        after(V, "v", [t_pr])
+        t_cn = done(V.tensor_reduce(out=col(T.cn, h), in_=T.pr[:, H[h]], axis=AxisListType.X, op=ALU.add))
+        after(V, "v", [t_cn, t_s[h], t_m[h]])
+        t_c.append(done(V.tensor_scalar(out=st(3, h), in0=st(1, h), scalar1=st(0, h), scalar2=col(T.cn, h),
+                                        op0=ALU.mult, op1=ALU.add)))
+    pack = t_m + t_m2 + t_s + t_c
+
+    direct, relay = _plan(core, T, topo)
+    after(g, "g", pack)
+    sent = 0
+    if relay:
+        sent += _send(g, core, T, topo, rank, [h for h, d in relay], _chip_mask(core, direct, relay, topo))
+    if direct:
+        sent += _send(g, core, T, topo, rank, direct, topo.mask(core, direct[0]))
+    total = 0
+    for p in T.cores:
+        if p == core:
+            continue
+        dp, rp = _plan(p, T, topo)
+        if core in dp:
+            total += _bits(topo.mask(p, core))
+        for h, dests in rp:
+            if core in dests:
+                total += _bits(topo.mask(h, dests[0]))
+    t_arr = (-1, T.sem.arr, total)
+
+    after(V, "v", t_m2)
+    t = done(V.tensor_scalar(out=T.a6[:], in0=T.land[:, rank, 2, :], scalar1=1.0 / 128, scalar2=6 * EPS,
+                             op0=ALU.mult, op1=ALU.add))
+    t_a6 = t
+    after(V, "v", [t])
+    t = done(V.reciprocal(T.ia6[:], T.a6[:]))
+    after(A, "a", [t])
+    t_y0 = done(A.activation(T.y0[:], T.ia6[:], ACT.Sqrt, scale=6.0))
+    after(V, "v", [t_y0])
+    t = done(V.tensor_tensor(out=T.y2[:], in0=T.y0[:], in1=T.y0[:], op=ALU.mult))
+    after(V, "v", [t])
+    t = done(V.tensor_tensor(out=T.ye[:], in0=T.y2[:], in1=T.a6[:], op=ALU.mult))
+    after(V, "v", [t])
+    t = done(V.tensor_scalar(out=T.yf[:], in0=T.ye[:], scalar1=-1.0 / 12, scalar2=1.5, op0=ALU.mult, op1=ALU.add))
+    after(V, "v", [t])
+    t = done(V.tensor_tensor(out=T.rsa[:], in0=T.y0[:], in1=T.yf[:], op=ALU.mult))
+    after(V, "v", [t, t_id])
+    t_ida = [done(V.tensor_scalar(out=T.ida[:, H[h]], in0=T.ident[:], scalar1=col(T.rsa, h), scalar2=None,
+                                  op0=ALU.mult)) for h in (0, 1)]
+
+    after(V, "v", [t_arr] + pack)
+    t = done(V.tensor_tensor(out=T.t3[:], in0=T.land[:, 0:3], in1=T.land[:, 3:6], op=ALU.add))
+    after(V, "v", [t])
+    t = done(V.tensor_tensor(out=T.t1[:], in0=T.t3[:, 0], in1=T.t3[:, 1], op=ALU.add))
+    after(V, "v", [t])
+    t_tot = done(V.tensor_tensor(out=T.tot[:], in0=T.t1[:], in1=T.t3[:, 2], op=ALU.add))
+    after(V, "v", [t_tot])
+    t_nmu = done(V.tensor_scalar(out=T.nmu[:], in0=T.tot[:, 0, :], scalar1=-1.0 / NR, scalar2=None, op0=ALU.mult))
+    after(A, "a", [t_nmu, t_arr] + t_m)
+    t_q = [done(A.activation(T.jq[:, 8 * h:8 * h + NR], T.land[:, :, 0, h], ACT.Square, bias=col(T.nmu, h),
+                             accum_out=col(T.sdd, h))) for h in (0, 1)]
+    after(A, "a", [t_tot])
+    t_na = done(A.activation(T.nega[:], T.tot[:, 1, :], ACT.Copy, scale=1.0 / NR))
+    after(A, "a", [t_na] + t_s)
+    t_dya = [done(A.activation(pd[h], pd[h], ACT.Identity, bias=col(T.nega, h))) for h in (0, 1)]
+    t_qm = done(V.tensor_scalar(out=T.qm[:], in0=T.tot[:, 2, :], scalar1=1.0 / 128, scalar2=6 * EPS,
+                                op0=ALU.mult, op1=ALU.add))
+    after(V, "v", [t_nmu])
+    t = done(V.tensor_tensor(out=T.tt[:], in0=T.nmu[:], in1=T.tot[:, 1, :], op=ALU.mult))
+    after(V, "v", [t])
+    t_ct = done(V.tensor_tensor(out=T.ct[:], in0=T.tt[:], in1=T.tot[:, 3, :], op=ALU.add))
+    after(V, "v", t_q + [t_qm])
+    t = done(V.tensor_tensor(out=T.v6[:], in0=T.sdd[:], in1=T.qm[:], op=ALU.add))
+    after(V, "v", [t])
+    t_iv = done(V.reciprocal(T.iv6[:], T.v6[:]))
+    after(V, "v", [t_iv, t_ct])
+    t_b = done(V.tensor_tensor(out=T.bb[:], in0=T.ct[:], in1=T.iv6[:], op=ALU.mult))
+
+    t_dg, t_v = [], []
+    for h in (0, 1):
+        after(A, "a", [t_iv, t_a6])
+        t = done(A.activation(col(T.r1, h), col(T.iv6, h), ACT.Sqrt, scale=col(T.a6, h)))
+        after(A, "a", [t, t_ida[h]])
+        t_dg.append(done(A.activation(T.dg[:, H[h]], T.ida[:, H[h]], ACT.Copy, scale=col(T.r1, h))))
+        after(V, "v", [t_b])
+        t = done(V.tensor_scalar(out=T.uu[:, H[h]], in0=px[h], scalar1=col(T.nmu, h), scalar2=col(T.bb, h),
+                                 op0=ALU.add, op1=ALU.mult))
+        after(V, "v", [t, t_dya[h]])
+        t_v.append(done(V.tensor_tensor(out=T.vv[:, H[h]], in0=T.uu[:, H[h]], in1=pd[h], op=ALU.add)))
+    t_mm = []
+    for h in (0, 1):
+        after(P, "p", [t_v[h], t_dg[h]])
+        t_mm.append(done(P.matmul(po[h], T.vv[:, H[h]], T.dg[:, H[h]], True, True)))
+    ist, sst = sem()
+    after(V, "v", [t_mm[0]])
+    t_c0 = done(V.tensor_copy(T.outs[:, H[0]], po[0]))
+    after(g.sync, "s", [t_c0])
+    g.sync.dma_start(T.dx[:, H[0]], T.outs[:, H[0]]).then_inc(sst, 16)
+    after(A, "a", [t_mm[1]])
+    t_c1 = done(A.activation(T.outs[:, H[1]], po[1], ACT.Copy))
+    after(A, "a", [t_c1])
+    A.dma_start(T.dx[:, H[1]], T.outs[:, H[1]]).then_inc(sst, 16)
+
+    g.wait_ge(T.sem.sent, sent)
+    g.wait_ge(sst, 32)

@@ -1,3 +1,4 @@
+import math
 from concourse.bass import DstId, RemoteDMATransfer
 from concourse.mybir import AluOpType, AxisListType, ActivationFunctionType
 
@@ -27,15 +28,18 @@ SCRATCH = {
     "yf": ("sbuf", [128, 2], "float32"),
     "rsa": ("sbuf", [128, 2], "float32"),
     "ida": ("sbuf", [128, 256], "float32"),
-    "t3": ("sbuf", [128, 3, 4, 2], "float32"),
-    "t1": ("sbuf", [128, 4, 2], "float32"),
-    "tot": ("sbuf", [128, 4, 2], "float32"),
+    "m3": ("sbuf", [128, 3, 2], "float32"),
+    "m1": ("sbuf", [128, 2], "float32"),
+    "ms": ("sbuf", [128, 2], "float32"),
     "nmu": ("sbuf", [128, 2], "float32"),
-    "qm": ("sbuf", [128, 2], "float32"),
-    "tt": ("sbuf", [128, 2], "float32"),
+    "sdd": ("sbuf", [128, 2], "float32"),
+    "sq6": ("sbuf", [128, 2], "float32"),
+    "xm": ("sbuf", [128, 256], "float32"),
+    "t3": ("sbuf", [128, 3, 3, 2], "float32"),
+    "t1": ("sbuf", [128, 3, 2], "float32"),
+    "tot": ("sbuf", [128, 3, 2], "float32"),
     "ct": ("sbuf", [128, 2], "float32"),
     "nega": ("sbuf", [128, 2], "float32"),
-    "sdd": ("sbuf", [128, 2], "float32"),
     "v6": ("sbuf", [128, 2], "float32"),
     "iv6": ("sbuf", [128, 2], "float32"),
     "bb": ("sbuf", [128, 2], "float32"),
@@ -51,7 +55,7 @@ SCRATCH = {
     "po0": ("psum", [128, 512], "float32"),
     "po1": ("psum", [128, 512], "float32"),
 }
-SEMAPHORES = ["arr", "sent"] + ["s%d" % i for i in range(NSEM)]
+SEMAPHORES = ["arr1", "arr2", "arrd", "sent"] + ["s%d" % i for i in range(NSEM)]
 
 
 def _bits(mask):
@@ -78,14 +82,14 @@ def _chip_mask(c, direct, relay, topo):
     return m
 
 
-def _send(g, core, T, topo, r, dests, mask):
+def _send(g, core, T, topo, piece, dests, mask, rsem):
     ids = []
     for d in dests:
         rid, pid = topo.addr(d, core)
         ids.append(DstId(rid=rid, pnc=pid))
     g.remote_dma_fused(
-        [RemoteDMATransfer(dst_ids=ids, dma_engine_mask=mask, remote_sem=T.sem.arr,
-                           srcs=[T.land[:, r]], dsts=[T.land[:, r] for d in dests], alu_op=0)],
+        [RemoteDMATransfer(dst_ids=ids, dma_engine_mask=mask, remote_sem=rsem,
+                           srcs=[piece], dsts=[piece for d in dests], alu_op=0)],
         local_sem=T.sem.sent)
     return _bits(mask)
 
@@ -97,8 +101,11 @@ def rank_program(g, core, T, topo):
             direct, relay = _plan(c, T, topo)
             for h, dests in relay:
                 if h == core:
-                    g.wait_ge(T.sem.arr, _bits(_chip_mask(c, direct, relay, topo)))
-                    n = _send(g, core, T, topo, r, dests, topo.mask(core, dests[0]))
+                    n_in = _bits(_chip_mask(c, direct, relay, topo))
+                    g.wait_ge(T.sem.arr1, n_in)
+                    n = _send(g, core, T, topo, T.land[:, r, 0, :], dests, topo.mask(core, dests[0]), T.sem.arr1)
+                    g.wait_ge(T.sem.arr2, n_in)
+                    n += _send(g, core, T, topo, T.land[:, r, 1:4, :], dests, topo.mask(core, dests[0]), T.sem.arr2)
                     g.wait_ge(T.sem.sent, n)
         return
 
@@ -159,7 +166,8 @@ def rank_program(g, core, T, topo):
         t_xc.append(done(V.tensor_scalar(out=T.xcs[:, H[h]], in0=px[h], scalar1=st(0, h), scalar2=-1.0 / 128,
                                          op0=ALU.subtract, op1=ALU.mult)))
         after(A, "a", [t_xc[h]])
-        t_m2.append(done(A.activation(T.j2[:, H[h]], T.xcs[:, H[h]], ACT.Square, scale=128.0, accum_out=st(2, h))))
+        t_m2.append(done(A.activation(T.j2[:, H[h]], T.xcs[:, H[h]], ACT.Square, scale=math.sqrt(128.0),
+                                      accum_out=st(2, h))))
     t_s, t_c = [], []
     for h in (0, 1):
         after(V, "v", [t_td[h], t_xc[h]])
@@ -171,32 +179,36 @@ def rank_program(g, core, T, topo):
         after(V, "v", [t_cn, t_s[h], t_m[h]])
         t_c.append(done(V.tensor_scalar(out=st(3, h), in0=st(1, h), scalar1=st(0, h), scalar2=col(T.cn, h),
                                         op0=ALU.mult, op1=ALU.add)))
-    pack = t_m + t_m2 + t_s + t_c
+    rest = t_m2 + t_s + t_c
 
     direct, relay = _plan(core, T, topo)
-    after(g, "g", pack)
+    helpers = [h for h, d in relay]
     sent = 0
     if relay:
-        sent += _send(g, core, T, topo, rank, [h for h, d in relay], _chip_mask(core, direct, relay, topo))
+        after(g, "g", t_m)
+        sent += _send(g, core, T, topo, T.land[:, rank, 0, :], helpers, _chip_mask(core, direct, relay, topo), T.sem.arr1)
+    after(g, "g", t_m + rest)
+    if relay:
+        sent += _send(g, core, T, topo, T.land[:, rank, 1:4, :], helpers, _chip_mask(core, direct, relay, topo),
+                      T.sem.arr2)
     if direct:
-        sent += _send(g, core, T, topo, rank, direct, topo.mask(core, direct[0]))
-    total = 0
+        sent += _send(g, core, T, topo, T.land[:, rank], direct, topo.mask(core, direct[0]), T.sem.arrd)
+    n_d, n_x = 0, 0
     for p in T.cores:
         if p == core:
             continue
         dp, rp = _plan(p, T, topo)
         if core in dp:
-            total += _bits(topo.mask(p, core))
+            n_d += _bits(topo.mask(p, core))
         for h, dests in rp:
             if core in dests:
-                total += _bits(topo.mask(h, dests[0]))
-    t_arr = (-1, T.sem.arr, total)
+                n_x += _bits(topo.mask(h, dests[0]))
+    t_means = [(-1, T.sem.arr1, n_x), (-2, T.sem.arrd, n_d)]
+    t_all = t_means + [(-3, T.sem.arr2, n_x)]
 
     after(V, "v", t_m2)
-    t = done(V.tensor_scalar(out=T.a6[:], in0=T.land[:, rank, 2, :], scalar1=1.0 / 128, scalar2=6 * EPS,
-                             op0=ALU.mult, op1=ALU.add))
-    t_a6 = t
-    after(V, "v", [t])
+    t_a6 = done(V.tensor_scalar(out=T.a6[:], in0=T.land[:, rank, 2, :], scalar1=6 * EPS, scalar2=None, op0=ALU.add))
+    after(V, "v", [t_a6])
     t = done(V.reciprocal(T.ia6[:], T.a6[:]))
     after(A, "a", [t])
     t_y0 = done(A.activation(T.y0[:], T.ia6[:], ACT.Sqrt, scale=6.0))
@@ -212,32 +224,36 @@ def rank_program(g, core, T, topo):
     t_ida = [done(V.tensor_scalar(out=T.ida[:, H[h]], in0=T.ident[:], scalar1=col(T.rsa, h), scalar2=None,
                                   op0=ALU.mult)) for h in (0, 1)]
 
-    after(V, "v", [t_arr] + pack)
-    t = done(V.tensor_tensor(out=T.t3[:], in0=T.land[:, 0:3], in1=T.land[:, 3:6], op=ALU.add))
+    after(V, "v", t_means + t_m)
+    t = done(V.tensor_tensor(out=T.m3[:], in0=T.land[:, 0:3, 0, :], in1=T.land[:, 3:6, 0, :], op=ALU.add))
+    after(V, "v", [t])
+    t = done(V.tensor_tensor(out=T.m1[:], in0=T.m3[:, 0, :], in1=T.m3[:, 1, :], op=ALU.add))
+    after(V, "v", [t])
+    t = done(V.tensor_tensor(out=T.ms[:], in0=T.m1[:], in1=T.m3[:, 2, :], op=ALU.add))
+    after(V, "v", [t])
+    t_nmu = done(V.tensor_scalar(out=T.nmu[:], in0=T.ms[:], scalar1=-1.0 / NR, scalar2=None, op0=ALU.mult))
+    after(A, "a", [t_nmu] + t_means + t_m)
+    t_q = [done(A.activation(T.jq[:, 8 * h:8 * h + NR], T.land[:, :, 0, h], ACT.Square, bias=col(T.nmu, h),
+                             accum_out=col(T.sdd, h))) for h in (0, 1)]
+    after(A, "a", t_q)
+    t_sq6 = done(A.activation(T.sq6[:], T.sdd[:], ACT.Identity, bias=6 * EPS))
+    t_xm = [done(A.activation(T.xm[:, H[h]], px[h], ACT.Identity, bias=col(T.nmu, h))) for h in (0, 1)]
+
+    after(V, "v", t_all + rest)
+    t = done(V.tensor_tensor(out=T.t3[:], in0=T.land[:, 0:3, 1:4, :], in1=T.land[:, 3:6, 1:4, :], op=ALU.add))
     after(V, "v", [t])
     t = done(V.tensor_tensor(out=T.t1[:], in0=T.t3[:, 0], in1=T.t3[:, 1], op=ALU.add))
     after(V, "v", [t])
     t_tot = done(V.tensor_tensor(out=T.tot[:], in0=T.t1[:], in1=T.t3[:, 2], op=ALU.add))
-    after(V, "v", [t_tot])
-    t_nmu = done(V.tensor_scalar(out=T.nmu[:], in0=T.tot[:, 0, :], scalar1=-1.0 / NR, scalar2=None, op0=ALU.mult))
-    after(A, "a", [t_nmu, t_arr] + t_m)
-    t_q = [done(A.activation(T.jq[:, 8 * h:8 * h + NR], T.land[:, :, 0, h], ACT.Square, bias=col(T.nmu, h),
-                             accum_out=col(T.sdd, h))) for h in (0, 1)]
-    after(A, "a", [t_tot])
-    t_na = done(A.activation(T.nega[:], T.tot[:, 1, :], ACT.Copy, scale=1.0 / NR))
-    after(A, "a", [t_na] + t_s)
-    t_dya = [done(A.activation(pd[h], pd[h], ACT.Identity, bias=col(T.nega, h))) for h in (0, 1)]
-    t_qm = done(V.tensor_scalar(out=T.qm[:], in0=T.tot[:, 2, :], scalar1=1.0 / 128, scalar2=6 * EPS,
-                                op0=ALU.mult, op1=ALU.add))
-    after(V, "v", [t_nmu])
-    t = done(V.tensor_tensor(out=T.tt[:], in0=T.nmu[:], in1=T.tot[:, 1, :], op=ALU.mult))
-    after(V, "v", [t])
-    t_ct = done(V.tensor_tensor(out=T.ct[:], in0=T.tt[:], in1=T.tot[:, 3, :], op=ALU.add))
-    after(V, "v", t_q + [t_qm])
-    t = done(V.tensor_tensor(out=T.v6[:], in0=T.sdd[:], in1=T.qm[:], op=ALU.add))
+    after(V, "v", [t_tot, t_sq6])
+    t = done(V.tensor_tensor(out=T.v6[:], in0=T.tot[:, 1, :], in1=T.sq6[:], op=ALU.add))
     after(V, "v", [t])
     t_iv = done(V.reciprocal(T.iv6[:], T.v6[:]))
-    after(V, "v", [t_iv, t_ct])
+    after(A, "a", [t_tot])
+    t_ct = [done(A.activation(col(T.ct, h), T.tot[:, 0, h:h + 1], ACT.Identity, bias=T.tot[:, 2, h:h + 1],
+                              scale=col(T.nmu, h))) for h in (0, 1)]
+    t_na = done(A.activation(T.nega[:], T.tot[:, 0, :], ACT.Copy, scale=1.0 / NR))
+    after(V, "v", [t_iv] + t_ct)
     t_b = done(V.tensor_tensor(out=T.bb[:], in0=T.ct[:], in1=T.iv6[:], op=ALU.mult))
 
     t_dg, t_v = [], []
@@ -246,10 +262,10 @@ def rank_program(g, core, T, topo):
         t = done(A.activation(col(T.r1, h), col(T.iv6, h), ACT.Sqrt, scale=col(T.a6, h)))
         after(A, "a", [t, t_ida[h]])
         t_dg.append(done(A.activation(T.dg[:, H[h]], T.ida[:, H[h]], ACT.Copy, scale=col(T.r1, h))))
-        after(V, "v", [t_b])
-        t = done(V.tensor_scalar(out=T.uu[:, H[h]], in0=px[h], scalar1=col(T.nmu, h), scalar2=col(T.bb, h),
-                                 op0=ALU.add, op1=ALU.mult))
-        after(V, "v", [t, t_dya[h]])
+        after(V, "v", [t_b, t_na, t_xm[h]])
+        t = done(V.tensor_scalar(out=T.uu[:, H[h]], in0=T.xm[:, H[h]], scalar1=col(T.bb, h), scalar2=col(T.nega, h),
+                                 op0=ALU.mult, op1=ALU.add))
+        after(V, "v", [t, t_s[h]])
         t_v.append(done(V.tensor_tensor(out=T.vv[:, H[h]], in0=T.uu[:, H[h]], in1=pd[h], op=ALU.add)))
     t_mm = []
     for h in (0, 1):

@@ -5,17 +5,17 @@ from concourse.mybir import AluOpType, AxisListType, ActivationFunctionType
 NSIM = 256
 NR = 6
 EPS = 0.01
-NSEM = 72
+NSEM = 76
 
 SCRATCH = {
     "xs": ("sbuf", [128, 256], "float32"),
     "dys": ("sbuf", [128, 256], "float32"),
     "ones": ("sbuf", [128, 128], "float32"),
+    "oc": ("sbuf", [128, 4], "float32"),
     "ident": ("sbuf", [128, 128], "float32"),
     "land": ("sbuf", [128, NR, 4, 2], "float32"),
     "xcs": ("sbuf", [128, 256], "float32"),
     "pr": ("sbuf", [128, 256], "float32"),
-    "j1": ("sbuf", [128, 256], "float32"),
     "j2": ("sbuf", [128, 256], "float32"),
     "j3": ("sbuf", [128, 256], "float32"),
     "jq": ("sbuf", [128, 16], "float32"),
@@ -28,15 +28,19 @@ SCRATCH = {
     "yf": ("sbuf", [128, 2], "float32"),
     "rsa": ("sbuf", [128, 2], "float32"),
     "ida": ("sbuf", [128, 256], "float32"),
-    "m3": ("sbuf", [128, 3, 2], "float32"),
-    "m1": ("sbuf", [128, 2], "float32"),
     "ms": ("sbuf", [128, 2], "float32"),
     "nmu": ("sbuf", [128, 2], "float32"),
     "sdd": ("sbuf", [128, 2], "float32"),
     "sq6": ("sbuf", [128, 2], "float32"),
     "xm": ("sbuf", [128, 256], "float32"),
-    "t3": ("sbuf", [128, 3, 3, 2], "float32"),
-    "t1": ("sbuf", [128, 3, 2], "float32"),
+    "w0": ("sbuf", [128, 2, 3, 2], "float32"),
+    "w1": ("sbuf", [128, 2, 3, 2], "float32"),
+    "w2": ("sbuf", [128, 2, 3, 2], "float32"),
+    "w3": ("sbuf", [128, 2, 3, 2], "float32"),
+    "w4": ("sbuf", [128, 2, 3, 2], "float32"),
+    "w5": ("sbuf", [128, 2, 3, 2], "float32"),
+    "w6": ("sbuf", [128, 2, 3, 2], "float32"),
+    "w7": ("sbuf", [128, 2, 3, 2], "float32"),
     "tot": ("sbuf", [128, 3, 2], "float32"),
     "ct": ("sbuf", [128, 2], "float32"),
     "nega": ("sbuf", [128, 2], "float32"),
@@ -54,8 +58,9 @@ SCRATCH = {
     "pd1": ("psum", [128, 512], "float32"),
     "po0": ("psum", [128, 512], "float32"),
     "po1": ("psum", [128, 512], "float32"),
+    "pm": ("psum", [128, 512], "float32"),
 }
-SEMAPHORES = ["arr1", "arr2", "arrd", "sent"] + ["s%d" % i for i in range(NSEM)]
+SEMAPHORES = ["arr1", "arr2", "ard1", "ard2", "sent"] + ["s%d" % i for i in range(NSEM)]
 
 
 def _bits(mask):
@@ -72,6 +77,13 @@ def _plan(c, T, topo):
     cand.sort(key=lambda k: (topo.die(k) != topo.die(c), k))
     relay = [(cand[i // 2], cross[i:i + 2]) for i in range(0, len(cross), 2)]
     return direct, relay
+
+
+def _slots(T, topo):
+    c0 = T.cores[0]
+    near = [c for c in T.cores if c == c0 or topo.may_write(c0, c)]
+    order = near + [c for c in T.cores if c not in near]
+    return dict((c, i) for i, c in enumerate(order))
 
 
 def _chip_mask(c, direct, relay, topo):
@@ -96,21 +108,24 @@ def _send(g, core, T, topo, piece, dests, mask, rsem):
 
 def rank_program(g, core, T, topo):
     rank = T.rank_of(core)
+    slot = _slots(T, topo)
     if rank is None:
-        for r, c in enumerate(T.cores):
+        for c in T.cores:
             direct, relay = _plan(c, T, topo)
             for h, dests in relay:
                 if h == core:
                     n_in = _bits(_chip_mask(c, direct, relay, topo))
+                    k = slot[c]
                     g.wait_ge(T.sem.arr1, n_in)
-                    n = _send(g, core, T, topo, T.land[:, r, 0, :], dests, topo.mask(core, dests[0]), T.sem.arr1)
+                    n = _send(g, core, T, topo, T.land[:, k, 0, :], dests, topo.mask(core, dests[0]), T.sem.arr1)
                     g.wait_ge(T.sem.arr2, n_in)
-                    n += _send(g, core, T, topo, T.land[:, r, 1:4, :], dests, topo.mask(core, dests[0]), T.sem.arr2)
+                    n += _send(g, core, T, topo, T.land[:, k, 1:4, :], dests, topo.mask(core, dests[0]), T.sem.arr2)
                     g.wait_ge(T.sem.sent, n)
         return
 
     V, A, P = g.vector, g.scalar, g.tensor
     ALU, ACT = AluOpType, ActivationFunctionType
+    own = slot[core]
     cnt = [0]
     seen = {}
 
@@ -134,35 +149,39 @@ def rank_program(g, core, T, topo):
         return t[:, h:h + 1]
 
     def st(k, h):
-        return T.land[:, rank, k, h:h + 1]
+        return T.land[:, own, k, h:h + 1]
 
     H = (slice(0, 128), slice(128, 256))
     px = (T.px0[:, 0:128], T.px1[:, 0:128])
     pd = (T.pd0[:, 0:128], T.pd1[:, 0:128])
     po = (T.po0[:, 0:128], T.po1[:, 0:128])
 
-    ix, sx = sem()
-    idy, sdy = sem()
-    g.sync.dma_start(T.xs[0:64, :], T.x[0:64, :]).then_inc(sx, 16)
-    A.dma_start(T.xs[64:128, :], T.x[64:128, :]).then_inc(sx, 16)
-    g.sync.dma_start(T.dys[0:64, :], T.dy[0:64, :]).then_inc(sdy, 16)
-    A.dma_start(T.dys[64:128, :], T.dy[64:128, :]).then_inc(sdy, 16)
-    t_x, t_dy = (ix, sx, 32), (idy, sdy, 32)
+    def load(dst, src):
+        i, s = sem()
+        g.sync.dma_start(dst[0:64, :], src[0:64, :]).then_inc(s, 16)
+        A.dma_start(dst[64:128, :], src[64:128, :]).then_inc(s, 16)
+        return (i, s, 32)
 
+    t_x = load(T.xs, T.x)
+    t_dy = load(T.dys, T.dy)
+
+    t_oc = done(V.memset(T.oc[:], 1.0 / 128))
     t_ones = done(V.memset(T.ones[:], 1.0))
     after(g, "g", [t_ones])
     t_id = done(g.affine_select(T.ident[:], T.ones[:], [[-1, 128]], ALU.is_equal, 0.0, 0, 1))
 
-    after(P, "p", [t_id, t_x])
+    after(P, "p", [t_oc, t_x])
+    t_pm = [done(P.matmul(T.pm[:, h:h + 1], T.xs[:, H[h]], T.oc[:, 0:1], True, True)) for h in (0, 1)]
+    after(V, "v", t_pm)
+    t_m = [done(V.tensor_copy(T.land[:, own, 0, :], T.pm[:, 0:2]))]
+    after(P, "p", [t_id])
     t_tx = [done(P.transpose(px[h], T.xs[:, H[h]], T.ident[:])) for h in (0, 1)]
     after(P, "p", [t_dy])
     t_td = [done(P.transpose(pd[h], T.dys[:, H[h]], T.ident[:])) for h in (0, 1)]
 
-    t_m, t_xc, t_m2 = [], [], []
+    t_xc, t_m2 = [], []
     for h in (0, 1):
-        after(A, "a", [t_tx[h]])
-        t_m.append(done(A.activation(T.j1[:, H[h]], px[h], ACT.Copy, scale=1.0 / 128, accum_out=st(0, h))))
-        after(V, "v", [t_m[h], t_tx[h]])
+        after(V, "v", t_m + [t_tx[h]])
         t_xc.append(done(V.tensor_scalar(out=T.xcs[:, H[h]], in0=px[h], scalar1=st(0, h), scalar2=-1.0 / 128,
                                          op0=ALU.subtract, op1=ALU.mult)))
         after(A, "a", [t_xc[h]])
@@ -176,7 +195,7 @@ def rank_program(g, core, T, topo):
         t_s.append(done(A.activation(T.j3[:, H[h]], pd[h], ACT.Copy, scale=-1.0 / 128, accum_out=st(1, h))))
         after(V, "v", [t_pr])
         t_cn = done(V.tensor_reduce(out=col(T.cn, h), in_=T.pr[:, H[h]], axis=AxisListType.X, op=ALU.add))
-        after(V, "v", [t_cn, t_s[h], t_m[h]])
+        after(V, "v", [t_cn, t_s[h]])
         t_c.append(done(V.tensor_scalar(out=st(3, h), in0=st(1, h), scalar1=st(0, h), scalar2=col(T.cn, h),
                                         op0=ALU.mult, op1=ALU.add)))
     rest = t_m2 + t_s + t_c
@@ -184,30 +203,52 @@ def rank_program(g, core, T, topo):
     direct, relay = _plan(core, T, topo)
     helpers = [h for h, d in relay]
     sent = 0
-    if relay:
-        after(g, "g", t_m)
-        sent += _send(g, core, T, topo, T.land[:, rank, 0, :], helpers, _chip_mask(core, direct, relay, topo), T.sem.arr1)
-    after(g, "g", t_m + rest)
-    if relay:
-        sent += _send(g, core, T, topo, T.land[:, rank, 1:4, :], helpers, _chip_mask(core, direct, relay, topo),
-                      T.sem.arr2)
-    if direct:
-        sent += _send(g, core, T, topo, T.land[:, rank], direct, topo.mask(core, direct[0]), T.sem.arrd)
+    for piece, deps, s_far, s_near in ((T.land[:, own, 0, :], t_m, T.sem.arr1, T.sem.ard1),
+                                       (T.land[:, own, 1:4, :], rest, T.sem.arr2, T.sem.ard2)):
+        after(g, "g", deps)
+        if relay:
+            sent += _send(g, core, T, topo, piece, helpers, _chip_mask(core, direct, relay, topo), s_far)
+        if direct:
+            sent += _send(g, core, T, topo, piece, direct, topo.mask(core, direct[0]), s_near)
     n_d, n_x = 0, 0
+    early, late = [own], []
     for p in T.cores:
         if p == core:
             continue
         dp, rp = _plan(p, T, topo)
         if core in dp:
             n_d += _bits(topo.mask(p, core))
+            early.append(slot[p])
         for h, dests in rp:
             if core in dests:
                 n_x += _bits(topo.mask(h, dests[0]))
-    t_means = [(-1, T.sem.arr1, n_x), (-2, T.sem.arrd, n_d)]
-    t_all = t_means + [(-3, T.sem.arr2, n_x)]
+                late.append(slot[p])
+    t_d1, t_d2 = [(-1, T.sem.ard1, n_d)], [(-2, T.sem.ard2, n_d)]
+    t_x1, t_x2 = [(-3, T.sem.arr1, n_x)], [(-4, T.sem.arr2, n_x)]
+
+    pool = [T.w0, T.w1, T.w2, T.w3, T.w4, T.w5, T.w6, T.w7]
+
+    def rsum(slots, deps, kl, kw):
+        s0, n = min(slots), len(slots)
+        after(V, "v", deps)
+        if n == 4:
+            w = pool.pop()
+            t = done(V.tensor_tensor(out=w[:, :, kw, :], in0=T.land[:, s0:s0 + 2, kl, :],
+                                     in1=T.land[:, s0 + 2:s0 + 4, kl, :], op=ALU.add))
+            parts = [w[:, 0, kw, :], w[:, 1, kw, :]]
+            after(V, "v", [t])
+        else:
+            parts = [T.land[:, s0 + i, kl, :] for i in range(n)]
+        acc, tok = parts[0], []
+        for p in parts[1:]:
+            w = pool.pop()
+            after(V, "v", tok)
+            tok = [done(V.tensor_tensor(out=w[:, 0, kw, :], in0=acc, in1=p, op=ALU.add))]
+            acc = w[:, 0, kw, :]
+        return acc, tok
 
     after(V, "v", t_m2)
-    t_a6 = done(V.tensor_scalar(out=T.a6[:], in0=T.land[:, rank, 2, :], scalar1=6 * EPS, scalar2=None, op0=ALU.add))
+    t_a6 = done(V.tensor_scalar(out=T.a6[:], in0=T.land[:, own, 2, :], scalar1=6 * EPS, scalar2=None, op0=ALU.add))
     after(V, "v", [t_a6])
     t = done(V.reciprocal(T.ia6[:], T.a6[:]))
     after(A, "a", [t])
@@ -224,27 +265,24 @@ def rank_program(g, core, T, topo):
     t_ida = [done(V.tensor_scalar(out=T.ida[:, H[h]], in0=T.ident[:], scalar1=col(T.rsa, h), scalar2=None,
                                   op0=ALU.mult)) for h in (0, 1)]
 
-    after(V, "v", t_means + t_m)
-    t = done(V.tensor_tensor(out=T.m3[:], in0=T.land[:, 0:3, 0, :], in1=T.land[:, 3:6, 0, :], op=ALU.add))
-    after(V, "v", [t])
-    t = done(V.tensor_tensor(out=T.m1[:], in0=T.m3[:, 0, :], in1=T.m3[:, 1, :], op=ALU.add))
-    after(V, "v", [t])
-    t = done(V.tensor_tensor(out=T.ms[:], in0=T.m1[:], in1=T.m3[:, 2, :], op=ALU.add))
+    me_ap, t_me = rsum(early, t_d1 + t_m, 0, 0)
+    ml_ap, t_ml = rsum(late, t_x1, 0, 0)
+    after(V, "v", t_me + t_ml)
+    t = done(V.tensor_tensor(out=T.ms[:], in0=ml_ap, in1=me_ap, op=ALU.add))
     after(V, "v", [t])
     t_nmu = done(V.tensor_scalar(out=T.nmu[:], in0=T.ms[:], scalar1=-1.0 / NR, scalar2=None, op0=ALU.mult))
-    after(A, "a", [t_nmu] + t_means + t_m)
+    after(A, "a", [t_nmu] + t_d1 + t_x1 + t_m)
     t_q = [done(A.activation(T.jq[:, 8 * h:8 * h + NR], T.land[:, :, 0, h], ACT.Square, bias=col(T.nmu, h),
                              accum_out=col(T.sdd, h))) for h in (0, 1)]
     after(A, "a", t_q)
     t_sq6 = done(A.activation(T.sq6[:], T.sdd[:], ACT.Identity, bias=6 * EPS))
+    after(A, "a", t_tx)
     t_xm = [done(A.activation(T.xm[:, H[h]], px[h], ACT.Identity, bias=col(T.nmu, h))) for h in (0, 1)]
 
-    after(V, "v", t_all + rest)
-    t = done(V.tensor_tensor(out=T.t3[:], in0=T.land[:, 0:3, 1:4, :], in1=T.land[:, 3:6, 1:4, :], op=ALU.add))
-    after(V, "v", [t])
-    t = done(V.tensor_tensor(out=T.t1[:], in0=T.t3[:, 0], in1=T.t3[:, 1], op=ALU.add))
-    after(V, "v", [t])
-    t_tot = done(V.tensor_tensor(out=T.tot[:], in0=T.t1[:], in1=T.t3[:, 2], op=ALU.add))
+    e_ap, t_e = rsum(early, t_d2 + rest, slice(1, 4), slice(0, 3))
+    l_ap, t_l = rsum(late, t_x2, slice(1, 4), slice(0, 3))
+    after(V, "v", t_l + t_e)
+    t_tot = done(V.tensor_tensor(out=T.tot[:], in0=l_ap, in1=e_ap, op=ALU.add))
     after(V, "v", [t_tot, t_sq6])
     t = done(V.tensor_tensor(out=T.v6[:], in0=T.tot[:, 1, :], in1=T.sq6[:], op=ALU.add))
     after(V, "v", [t])

@@ -5,7 +5,7 @@ from concourse.mybir import AluOpType, AxisListType, ActivationFunctionType
 NSIM = 256
 NR = 6
 EPS = 0.01
-NSEM = 76
+NSEM = 90
 
 SCRATCH = {
     "xs": ("sbuf", [128, 256], "float32"),
@@ -18,7 +18,8 @@ SCRATCH = {
     "pr": ("sbuf", [128, 256], "float32"),
     "j2": ("sbuf", [128, 256], "float32"),
     "j3": ("sbuf", [128, 256], "float32"),
-    "jq": ("sbuf", [128, 16], "float32"),
+    "jq": ("sbuf", [128, 8, 8], "float32"),
+    "m6": ("sbuf", [128, 2], "float32"),
     "cn": ("sbuf", [128, 2], "float32"),
     "a6": ("sbuf", [128, 2], "float32"),
     "ia6": ("sbuf", [128, 2], "float32"),
@@ -28,10 +29,9 @@ SCRATCH = {
     "yf": ("sbuf", [128, 2], "float32"),
     "rsa": ("sbuf", [128, 2], "float32"),
     "ida": ("sbuf", [128, 256], "float32"),
-    "ms": ("sbuf", [128, 2], "float32"),
     "nmu": ("sbuf", [128, 2], "float32"),
+    "nms": ("sbuf", [128, 2], "float32"),
     "sdd": ("sbuf", [128, 2], "float32"),
-    "sq6": ("sbuf", [128, 2], "float32"),
     "xm": ("sbuf", [128, 256], "float32"),
     "w0": ("sbuf", [128, 2, 3, 2], "float32"),
     "w1": ("sbuf", [128, 2, 3, 2], "float32"),
@@ -39,14 +39,9 @@ SCRATCH = {
     "w3": ("sbuf", [128, 2, 3, 2], "float32"),
     "w4": ("sbuf", [128, 2, 3, 2], "float32"),
     "w5": ("sbuf", [128, 2, 3, 2], "float32"),
-    "w6": ("sbuf", [128, 2, 3, 2], "float32"),
-    "w7": ("sbuf", [128, 2, 3, 2], "float32"),
     "tot": ("sbuf", [128, 3, 2], "float32"),
     "ct": ("sbuf", [128, 2], "float32"),
-    "nega": ("sbuf", [128, 2], "float32"),
-    "v6": ("sbuf", [128, 2], "float32"),
     "iv6": ("sbuf", [128, 2], "float32"),
-    "bb": ("sbuf", [128, 2], "float32"),
     "r1": ("sbuf", [128, 2], "float32"),
     "dg": ("sbuf", [128, 256], "float32"),
     "uu": ("sbuf", [128, 256], "float32"),
@@ -58,6 +53,7 @@ SCRATCH = {
     "pd1": ("psum", [128, 512], "float32"),
     "po0": ("psum", [128, 512], "float32"),
     "po1": ("psum", [128, 512], "float32"),
+    "po2": ("psum", [128, 512], "float32"),
     "pm": ("psum", [128, 512], "float32"),
 }
 SEMAPHORES = ["arr1", "arr2", "ard1", "ard2", "sent"] + ["s%d" % i for i in range(NSEM)]
@@ -134,10 +130,10 @@ def rank_program(g, core, T, topo):
         cnt[0] += 1
         return i, T.sem["s%d" % i]
 
-    def done(instr):
+    def done(instr, n=1):
         i, s = sem()
-        instr.then_inc(s, 1)
-        return (i, s, 1)
+        instr.then_inc(s, n)
+        return (i, s, n)
 
     def after(q, qn, toks):
         for (i, s, v) in toks:
@@ -154,30 +150,29 @@ def rank_program(g, core, T, topo):
     H = (slice(0, 128), slice(128, 256))
     px = (T.px0[:, 0:128], T.px1[:, 0:128])
     pd = (T.pd0[:, 0:128], T.pd1[:, 0:128])
-    po = (T.po0[:, 0:128], T.po1[:, 0:128])
 
-    def load(dst, src):
-        i, s = sem()
-        g.sync.dma_start(dst[0:64, :], src[0:64, :]).then_inc(s, 16)
-        A.dma_start(dst[64:128, :], src[64:128, :]).then_inc(s, 16)
-        return (i, s, 32)
-
-    t_x = load(T.xs, T.x)
-    t_dy = load(T.dys, T.dy)
+    Q = (g.sync, A)
+    t_x = [done(Q[h].dma_start(T.xs[:, H[h]], T.x[:, H[h]]), 16) for h in (0, 1)]
+    t_dy = [done(Q[h].dma_start(T.dys[:, H[h]], T.dy[:, H[h]]), 16) for h in (0, 1)]
 
     t_oc = done(V.memset(T.oc[:], 1.0 / 128))
     t_ones = done(V.memset(T.ones[:], 1.0))
     after(g, "g", [t_ones])
     t_id = done(g.affine_select(T.ident[:], T.ones[:], [[-1, 128]], ALU.is_equal, 0.0, 0, 1))
 
-    after(P, "p", [t_oc, t_x])
-    t_pm = [done(P.matmul(T.pm[:, h:h + 1], T.xs[:, H[h]], T.oc[:, 0:1], True, True)) for h in (0, 1)]
+    t_pm = []
+    for h in (0, 1):
+        after(P, "p", [t_oc, t_x[h]])
+        t_pm.append(done(P.matmul(T.pm[:, h:h + 1], T.xs[:, H[h]], T.oc[:, 0:1], True, True)))
     after(V, "v", t_pm)
     t_m = [done(V.tensor_copy(T.land[:, own, 0, :], T.pm[:, 0:2]))]
+    t_m6 = done(V.tensor_scalar(out=T.m6[:], in0=T.pm[:, 0:2], scalar1=6.0, scalar2=None, op0=ALU.mult))
     after(P, "p", [t_id])
     t_tx = [done(P.transpose(px[h], T.xs[:, H[h]], T.ident[:])) for h in (0, 1)]
-    after(P, "p", [t_dy])
-    t_td = [done(P.transpose(pd[h], T.dys[:, H[h]], T.ident[:])) for h in (0, 1)]
+    t_td = []
+    for h in (0, 1):
+        after(P, "p", [t_dy[h]])
+        t_td.append(done(P.transpose(pd[h], T.dys[:, H[h]], T.ident[:])))
 
     t_xc, t_m2 = [], []
     for h in (0, 1):
@@ -192,11 +187,11 @@ def rank_program(g, core, T, topo):
         after(V, "v", [t_td[h], t_xc[h]])
         t_pr = done(V.tensor_tensor(out=T.pr[:, H[h]], in0=pd[h], in1=T.xcs[:, H[h]], op=ALU.mult))
         after(A, "a", [t_pr, t_td[h]])
-        t_s.append(done(A.activation(T.j3[:, H[h]], pd[h], ACT.Copy, scale=-1.0 / 128, accum_out=st(1, h))))
+        t_s.append(done(A.activation(T.j3[:, H[h]], pd[h], ACT.Copy, scale=-1.0 / (128 * NR), accum_out=st(1, h))))
         after(V, "v", [t_pr])
         t_cn = done(V.tensor_reduce(out=col(T.cn, h), in_=T.pr[:, H[h]], axis=AxisListType.X, op=ALU.add))
-        after(V, "v", [t_cn, t_s[h]])
-        t_c.append(done(V.tensor_scalar(out=st(3, h), in0=st(1, h), scalar1=st(0, h), scalar2=col(T.cn, h),
+        after(V, "v", [t_cn, t_s[h], t_m6])
+        t_c.append(done(V.tensor_scalar(out=st(3, h), in0=st(1, h), scalar1=col(T.m6, h), scalar2=col(T.cn, h),
                                         op0=ALU.mult, op1=ALU.add)))
     rest = t_m2 + t_s + t_c
 
@@ -226,26 +221,26 @@ def rank_program(g, core, T, topo):
     t_d1, t_d2 = [(-1, T.sem.ard1, n_d)], [(-2, T.sem.ard2, n_d)]
     t_x1, t_x2 = [(-3, T.sem.arr1, n_x)], [(-4, T.sem.arr2, n_x)]
 
-    pool = [T.w0, T.w1, T.w2, T.w3, T.w4, T.w5, T.w6, T.w7]
+    pool = [T.w0, T.w1, T.w2, T.w3, T.w4, T.w5]
 
-    def rsum(slots, deps, kl, kw):
+    def rsum(slots, deps):
         s0, n = min(slots), len(slots)
         after(V, "v", deps)
         if n == 4:
             w = pool.pop()
-            t = done(V.tensor_tensor(out=w[:, :, kw, :], in0=T.land[:, s0:s0 + 2, kl, :],
-                                     in1=T.land[:, s0 + 2:s0 + 4, kl, :], op=ALU.add))
-            parts = [w[:, 0, kw, :], w[:, 1, kw, :]]
+            t = done(V.tensor_tensor(out=w[:], in0=T.land[:, s0:s0 + 2, 1:4, :],
+                                     in1=T.land[:, s0 + 2:s0 + 4, 1:4, :], op=ALU.add))
+            parts = [w[:, 0, :, :], w[:, 1, :, :]]
             after(V, "v", [t])
         else:
-            parts = [T.land[:, s0 + i, kl, :] for i in range(n)]
-        acc, tok = parts[0], []
+            parts = [T.land[:, s0 + i, 1:4, :] for i in range(n)]
+        acc, tok, w = parts[0], [], None
         for p in parts[1:]:
             w = pool.pop()
             after(V, "v", tok)
-            tok = [done(V.tensor_tensor(out=w[:, 0, kw, :], in0=acc, in1=p, op=ALU.add))]
-            acc = w[:, 0, kw, :]
-        return acc, tok
+            tok = [done(V.tensor_tensor(out=w[:, 0, :, :], in0=acc, in1=p, op=ALU.add))]
+            acc = w[:, 0, :, :]
+        return w, tok
 
     after(V, "v", t_m2)
     t_a6 = done(V.tensor_scalar(out=T.a6[:], in0=T.land[:, own, 2, :], scalar1=6 * EPS, scalar2=None, op0=ALU.add))
@@ -265,59 +260,62 @@ def rank_program(g, core, T, topo):
     t_ida = [done(V.tensor_scalar(out=T.ida[:, H[h]], in0=T.ident[:], scalar1=col(T.rsa, h), scalar2=None,
                                   op0=ALU.mult)) for h in (0, 1)]
 
-    me_ap, t_me = rsum(early, t_d1 + t_m, 0, 0)
-    ml_ap, t_ml = rsum(late, t_x1, 0, 0)
-    after(V, "v", t_me + t_ml)
-    t = done(V.tensor_tensor(out=T.ms[:], in0=ml_ap, in1=me_ap, op=ALU.add))
-    after(V, "v", [t])
-    t_nmu = done(V.tensor_scalar(out=T.nmu[:], in0=T.ms[:], scalar1=-1.0 / NR, scalar2=None, op0=ALU.mult))
-    after(A, "a", [t_nmu] + t_d1 + t_x1 + t_m)
-    t_q = [done(A.activation(T.jq[:, 8 * h:8 * h + NR], T.land[:, :, 0, h], ACT.Square, bias=col(T.nmu, h),
+    after(A, "a", t_d1 + t_x1 + t_m)
+    t_nmu = [done(A.activation(T.jq[:, h, 0:NR], T.land[:, :, 0, h], ACT.Copy, scale=-1.0 / NR,
+                               accum_out=col(T.nmu, h))) for h in (0, 1)]
+    after(A, "a", t_nmu)
+    t_q = [done(A.activation(T.jq[:, 2 + h, 0:NR], T.land[:, :, 0, h], ACT.Square, bias=col(T.nmu, h),
                              accum_out=col(T.sdd, h))) for h in (0, 1)]
-    after(A, "a", t_q)
-    t_sq6 = done(A.activation(T.sq6[:], T.sdd[:], ACT.Identity, bias=6 * EPS))
     after(A, "a", t_tx)
     t_xm = [done(A.activation(T.xm[:, H[h]], px[h], ACT.Identity, bias=col(T.nmu, h))) for h in (0, 1)]
+    t_nms = [done(A.activation(T.jq[:, 4 + h, 0:NR], T.land[:, :, 0, h], ACT.Copy, scale=-1.0,
+                               accum_out=col(T.nms, h))) for h in (0, 1)]
 
-    e_ap, t_e = rsum(early, t_d2 + rest, slice(1, 4), slice(0, 3))
-    l_ap, t_l = rsum(late, t_x2, slice(1, 4), slice(0, 3))
-    after(V, "v", t_l + t_e)
-    t_tot = done(V.tensor_tensor(out=T.tot[:], in0=l_ap, in1=e_ap, op=ALU.add))
-    after(V, "v", [t_tot, t_sq6])
-    t = done(V.tensor_tensor(out=T.v6[:], in0=T.tot[:, 1, :], in1=T.sq6[:], op=ALU.add))
-    after(V, "v", [t])
-    t_iv = done(V.reciprocal(T.iv6[:], T.v6[:]))
-    after(A, "a", [t_tot])
-    t_ct = [done(A.activation(col(T.ct, h), T.tot[:, 0, h:h + 1], ACT.Identity, bias=T.tot[:, 2, h:h + 1],
-                              scale=col(T.nmu, h))) for h in (0, 1)]
-    t_na = done(A.activation(T.nega[:], T.tot[:, 0, :], ACT.Copy, scale=1.0 / NR))
-    after(V, "v", [t_iv] + t_ct)
-    t_b = done(V.tensor_tensor(out=T.bb[:], in0=T.ct[:], in1=T.iv6[:], op=ALU.mult))
+    we, t_e = rsum(early, t_d2 + rest)
+    after(V, "v", t_e)
+    t = done(V.tensor_scalar(out=we[:, 0, 1, :], in0=we[:, 0, 1, :], scalar1=6 * EPS, scalar2=None, op0=ALU.add))
+    after(V, "v", [t] + t_q)
+    t_e2 = done(V.tensor_tensor(out=we[:, 0, 1, :], in0=we[:, 0, 1, :], in1=T.sdd[:], op=ALU.add))
+    wl, t_l = rsum(late, t_x2)
+    after(V, "v", t_l + [t_e2])
+    t_tot = done(V.tensor_tensor(out=T.tot[:], in0=wl[:, 0, :, :], in1=we[:, 0, :, :], op=ALU.add))
+    after(V, "v", [t_tot])
+    t_iv = done(V.reciprocal(T.iv6[:], T.tot[:, 1, :]))
 
     t_dg, t_v = [], []
     for h in (0, 1):
+        after(A, "a", [t_tot, t_nms[h]])
+        t_ct = done(A.activation(col(T.ct, h), T.tot[:, 0, h:h + 1], ACT.Identity, bias=T.tot[:, 2, h:h + 1],
+                                 scale=col(T.nms, h)))
+        after(A, "a", [t_s[h]])
+        t_da = done(A.activation(pd[h], pd[h], ACT.Identity, bias=T.tot[:, 0, h:h + 1]))
         after(A, "a", [t_iv, t_a6])
         t = done(A.activation(col(T.r1, h), col(T.iv6, h), ACT.Sqrt, scale=col(T.a6, h)))
         after(A, "a", [t, t_ida[h]])
         t_dg.append(done(A.activation(T.dg[:, H[h]], T.ida[:, H[h]], ACT.Copy, scale=col(T.r1, h))))
-        after(V, "v", [t_b, t_na, t_xm[h]])
-        t = done(V.tensor_scalar(out=T.uu[:, H[h]], in0=T.xm[:, H[h]], scalar1=col(T.bb, h), scalar2=col(T.nega, h),
-                                 op0=ALU.mult, op1=ALU.add))
-        after(V, "v", [t, t_s[h]])
+        after(V, "v", [t_iv, t_ct, t_xm[h]])
+        t = done(V.tensor_scalar(out=T.uu[:, H[h]], in0=T.xm[:, H[h]], scalar1=col(T.iv6, h), scalar2=col(T.ct, h),
+                                 op0=ALU.mult, op1=ALU.mult))
+        after(V, "v", [t, t_da])
         t_v.append(done(V.tensor_tensor(out=T.vv[:, H[h]], in0=T.uu[:, H[h]], in1=pd[h], op=ALU.add)))
+
+    pieces = ((0, slice(0, 128), T.po0[:, 0:128]), (1, slice(128, 192), T.po1[:, 0:64]), (1, slice(192, 256), T.po2[:, 0:64]))
     t_mm = []
-    for h in (0, 1):
+    for h, cs, po in pieces:
         after(P, "p", [t_v[h], t_dg[h]])
-        t_mm.append(done(P.matmul(po[h], T.vv[:, H[h]], T.dg[:, H[h]], True, True)))
+        t_mm.append(done(P.matmul(po, T.vv[:, H[h]], T.dg[:, cs], True, True)))
     ist, sst = sem()
-    after(V, "v", [t_mm[0]])
-    t_c0 = done(V.tensor_copy(T.outs[:, H[0]], po[0]))
-    after(g.sync, "s", [t_c0])
-    g.sync.dma_start(T.dx[:, H[0]], T.outs[:, H[0]]).then_inc(sst, 16)
-    after(A, "a", [t_mm[1]])
-    t_c1 = done(A.activation(T.outs[:, H[1]], po[1], ACT.Copy))
-    after(A, "a", [t_c1])
-    A.dma_start(T.dx[:, H[1]], T.outs[:, H[1]]).then_inc(sst, 16)
+    for i in (0, 1):
+        h, cs, po = pieces[i]
+        after(V, "v", [t_mm[i]])
+        t_cp = done(V.tensor_copy(T.outs[:, cs], po))
+        after(g.sync, "s", [t_cp])
+        g.sync.dma_start(T.dx[:, cs], T.outs[:, cs]).then_inc(sst, 16)
+    h, cs, po = pieces[2]
+    after(A, "a", [t_mm[2]])
+    t_cp = done(A.activation(T.outs[:, cs], po, ACT.Copy))
+    after(A, "a", [t_cp])
+    A.dma_start(T.dx[:, cs], T.outs[:, cs]).then_inc(sst, 16)
 
     g.wait_ge(T.sem.sent, sent)
-    g.wait_ge(sst, 32)
+    g.wait_ge(sst, 48)

@@ -12,36 +12,26 @@ SCRATCH = {
     "dys": ("sbuf", [128, 256], "float32"),
     "ones": ("sbuf", [128, 128], "float32"),
     "oc": ("sbuf", [128, 4], "float32"),
+    "six": ("sbuf", [128, 4], "float32"),
+    "c6": ("sbuf", [128, 4], "float32"),
     "ident": ("sbuf", [128, 128], "float32"),
-    "land": ("sbuf", [128, NR, 4, 2], "float32"),
-    "xcs": ("sbuf", [128, 256], "float32"),
+    "ida": ("sbuf", [128, 128], "float32"),
+    "landm": ("sbuf", [128, NR, 4], "float32"),
+    "land": ("sbuf", [128, NR + 2, 8], "float32"),
+    "xts": ("sbuf", [128, 256], "float32"),
     "pr": ("sbuf", [128, 256], "float32"),
     "j2": ("sbuf", [128, 256], "float32"),
     "j3": ("sbuf", [128, 256], "float32"),
-    "jq": ("sbuf", [128, 8, 8], "float32"),
-    "m6": ("sbuf", [128, 2], "float32"),
-    "cn": ("sbuf", [128, 2], "float32"),
-    "a6": ("sbuf", [128, 2], "float32"),
-    "ia6": ("sbuf", [128, 2], "float32"),
-    "y0": ("sbuf", [128, 2], "float32"),
-    "y2": ("sbuf", [128, 2], "float32"),
-    "ye": ("sbuf", [128, 2], "float32"),
-    "yf": ("sbuf", [128, 2], "float32"),
-    "rsa": ("sbuf", [128, 2], "float32"),
-    "ida": ("sbuf", [128, 256], "float32"),
+    "jq": ("sbuf", [128, 12, 8], "float32"),
+    "nb": ("sbuf", [128, 2], "float32"),
     "nmu": ("sbuf", [128, 2], "float32"),
     "nms": ("sbuf", [128, 2], "float32"),
-    "sdd": ("sbuf", [128, 2], "float32"),
     "xm": ("sbuf", [128, 256], "float32"),
-    "w0": ("sbuf", [128, 2, 3, 2], "float32"),
-    "w1": ("sbuf", [128, 2, 3, 2], "float32"),
-    "w2": ("sbuf", [128, 2, 3, 2], "float32"),
-    "w3": ("sbuf", [128, 2, 3, 2], "float32"),
-    "w4": ("sbuf", [128, 2, 3, 2], "float32"),
-    "w5": ("sbuf", [128, 2, 3, 2], "float32"),
-    "tot": ("sbuf", [128, 3, 2], "float32"),
-    "ct": ("sbuf", [128, 2], "float32"),
+    "v6": ("sbuf", [128, 2], "float32"),
     "iv6": ("sbuf", [128, 2], "float32"),
+    "na": ("sbuf", [128, 2], "float32"),
+    "sc": ("sbuf", [128, 2], "float32"),
+    "ct": ("sbuf", [128, 2], "float32"),
     "r1": ("sbuf", [128, 2], "float32"),
     "dg": ("sbuf", [128, 256], "float32"),
     "uu": ("sbuf", [128, 256], "float32"),
@@ -56,7 +46,7 @@ SCRATCH = {
     "po2": ("psum", [128, 512], "float32"),
     "pm": ("psum", [128, 512], "float32"),
 }
-SEMAPHORES = ["arr1", "arr2", "ard1", "ard2", "sent"] + ["s%d" % i for i in range(NSEM)]
+SEMAPHORES = ["arr1", "arr2", "arr3", "ard1", "ard2", "ard3", "sent"] + ["s%d" % i for i in range(NSEM)]
 
 
 def _bits(mask):
@@ -73,13 +63,6 @@ def _plan(c, T, topo):
     cand.sort(key=lambda k: (topo.die(k) != topo.die(c), k))
     relay = [(cand[i // 2], cross[i:i + 2]) for i in range(0, len(cross), 2)]
     return direct, relay
-
-
-def _slots(T, topo):
-    c0 = T.cores[0]
-    near = [c for c in T.cores if c == c0 or topo.may_write(c0, c)]
-    order = near + [c for c in T.cores if c not in near]
-    return dict((c, i) for i, c in enumerate(order))
 
 
 def _chip_mask(c, direct, relay, topo):
@@ -102,28 +85,35 @@ def _send(g, core, T, topo, piece, dests, mask, rsem):
     return _bits(mask)
 
 
+def _pieces(T, k):
+    return (T.landm[:, k, 0:2], T.land[:, k, 0:3], T.land[:, k, 3:6])
+
+
 def rank_program(g, core, T, topo):
     rank = T.rank_of(core)
-    slot = _slots(T, topo)
+    far = (T.sem.arr1, T.sem.arr2, T.sem.arr3)
+    near = (T.sem.ard1, T.sem.ard2, T.sem.ard3)
     if rank is None:
         for c in T.cores:
             direct, relay = _plan(c, T, topo)
             for h, dests in relay:
                 if h == core:
                     n_in = _bits(_chip_mask(c, direct, relay, topo))
-                    k = slot[c]
-                    g.wait_ge(T.sem.arr1, n_in)
-                    n = _send(g, core, T, topo, T.land[:, k, 0, :], dests, topo.mask(core, dests[0]), T.sem.arr1)
-                    g.wait_ge(T.sem.arr2, n_in)
-                    n += _send(g, core, T, topo, T.land[:, k, 1:4, :], dests, topo.mask(core, dests[0]), T.sem.arr2)
+                    n = 0
+                    for piece, s in zip(_pieces(T, T.rank_of(c)), far):
+                        g.wait_ge(s, n_in)
+                        n += _send(g, core, T, topo, piece, dests, topo.mask(core, dests[0]), s)
                     g.wait_ge(T.sem.sent, n)
         return
 
     V, A, P = g.vector, g.scalar, g.tensor
     ALU, ACT = AluOpType, ActivationFunctionType
-    own = slot[core]
+    own = rank
+    E1, E2 = NR, NR + 1
     cnt = [0]
     seen = {}
+    waited = {}
+    made = []
 
     def sem():
         i = cnt[0]
@@ -133,10 +123,12 @@ def rank_program(g, core, T, topo):
     def done(instr, n=1):
         i, s = sem()
         instr.then_inc(s, n)
+        made.append((i, s, n))
         return (i, s, n)
 
     def after(q, qn, toks):
         for (i, s, v) in toks:
+            waited[i] = True
             if (qn, i) not in seen:
                 seen[(qn, i)] = True
                 q.wait_ge(s, v)
@@ -145,7 +137,7 @@ def rank_program(g, core, T, topo):
         return t[:, h:h + 1]
 
     def st(k, h):
-        return T.land[:, own, k, h:h + 1]
+        return T.land[:, own, 3 * h + k:3 * h + k + 1]
 
     H = (slice(0, 128), slice(128, 256))
     px = (T.px0[:, 0:128], T.px1[:, 0:128])
@@ -155,154 +147,149 @@ def rank_program(g, core, T, topo):
     t_x = [done(Q[h].dma_start(T.xs[:, H[h]], T.x[:, H[h]]), 16) for h in (0, 1)]
     t_dy = [done(Q[h].dma_start(T.dys[:, H[h]], T.dy[:, H[h]]), 16) for h in (0, 1)]
 
+    t_six = done(V.memset(T.six[:], 6.0))
     t_oc = done(V.memset(T.oc[:], 1.0 / 128))
     t_ones = done(V.memset(T.ones[:], 1.0))
+    t_eps = [done(V.memset(T.land[:, E2, 3 * h + 1:3 * h + 2], 6 * EPS)) for h in (0, 1)]
     after(g, "g", [t_ones])
     t_id = done(g.affine_select(T.ident[:], T.ones[:], [[-1, 128]], ALU.is_equal, 0.0, 0, 1))
+    after(A, "a", [t_six])
+    t_c6 = done(A.activation(T.c6[:], T.six[:], ACT.Sqrt))
+    after(A, "a", [t_c6, t_id])
+    t_ida = done(A.activation(T.ida[:], T.ident[:], ACT.Copy, scale=T.c6[:, 0:1]))
 
     t_pm = []
     for h in (0, 1):
         after(P, "p", [t_oc, t_x[h]])
         t_pm.append(done(P.matmul(T.pm[:, h:h + 1], T.xs[:, H[h]], T.oc[:, 0:1], True, True)))
     after(V, "v", t_pm)
-    t_m = [done(V.tensor_copy(T.land[:, own, 0, :], T.pm[:, 0:2]))]
-    t_m6 = done(V.tensor_scalar(out=T.m6[:], in0=T.pm[:, 0:2], scalar1=6.0, scalar2=None, op0=ALU.mult))
+    t_m = done(V.tensor_copy(T.landm[:, own, 0:2], T.pm[:, 0:2]))
+    t_nb = done(V.tensor_scalar(out=T.nb[:], in0=T.pm[:, 0:2], scalar1=-1.0 / math.sqrt(128.0), scalar2=None, op0=ALU.mult))
     after(P, "p", [t_id])
-    t_tx = [done(P.transpose(px[h], T.xs[:, H[h]], T.ident[:])) for h in (0, 1)]
-    t_td = []
+    t_tx, t_td = [], []
     for h in (0, 1):
+        t_tx.append(done(P.transpose(px[h], T.xs[:, H[h]], T.ident[:])))
         after(P, "p", [t_dy[h]])
         t_td.append(done(P.transpose(pd[h], T.dys[:, H[h]], T.ident[:])))
 
-    t_xc, t_m2 = [], []
+    t_xt, t_m2, t_s, t_c = [], [], [], []
     for h in (0, 1):
-        after(V, "v", t_m + [t_tx[h]])
-        t_xc.append(done(V.tensor_scalar(out=T.xcs[:, H[h]], in0=px[h], scalar1=st(0, h), scalar2=-1.0 / 128,
-                                         op0=ALU.subtract, op1=ALU.mult)))
-        after(A, "a", [t_xc[h]])
-        t_m2.append(done(A.activation(T.j2[:, H[h]], T.xcs[:, H[h]], ACT.Square, scale=math.sqrt(128.0),
-                                      accum_out=st(2, h))))
-    t_s, t_c = [], []
-    for h in (0, 1):
-        after(V, "v", [t_td[h], t_xc[h]])
-        t_pr = done(V.tensor_tensor(out=T.pr[:, H[h]], in0=pd[h], in1=T.xcs[:, H[h]], op=ALU.mult))
+        after(V, "v", [t_tx[h]])
+        t_xt.append(done(V.tensor_scalar(out=T.xts[:, H[h]], in0=px[h], scalar1=-1.0 / 128, scalar2=None, op0=ALU.mult)))
+        after(A, "a", [t_xt[h], t_nb])
+        t_m2.append(done(A.activation(T.j2[:, H[h]], T.xts[:, H[h]], ACT.Square, scale=-math.sqrt(128.0), bias=col(T.nb, h),
+                                      accum_out=st(1, h))))
+        after(V, "v", [t_td[h], t_xt[h]])
+        t_pr = done(V.tensor_tensor(out=T.pr[:, H[h]], in0=pd[h], in1=T.xts[:, H[h]], op=ALU.mult))
         after(A, "a", [t_pr, t_td[h]])
-        t_s.append(done(A.activation(T.j3[:, H[h]], pd[h], ACT.Copy, scale=-1.0 / (128 * NR), accum_out=st(1, h))))
+        t_s.append(done(A.activation(T.j3[:, H[h]], pd[h], ACT.Copy, scale=-1.0 / (128 * NR), accum_out=st(0, h))))
         after(V, "v", [t_pr])
-        t_cn = done(V.tensor_reduce(out=col(T.cn, h), in_=T.pr[:, H[h]], axis=AxisListType.X, op=ALU.add))
-        after(V, "v", [t_cn, t_s[h], t_m6])
-        t_c.append(done(V.tensor_scalar(out=st(3, h), in0=st(1, h), scalar1=col(T.m6, h), scalar2=col(T.cn, h),
-                                        op0=ALU.mult, op1=ALU.add)))
-    rest = t_m2 + t_s + t_c
+        t_c.append(done(V.tensor_reduce(out=st(2, h), in_=T.pr[:, H[h]], axis=AxisListType.X, op=ALU.add)))
 
     direct, relay = _plan(core, T, topo)
     helpers = [h for h, d in relay]
     sent = 0
-    for piece, deps, s_far, s_near in ((T.land[:, own, 0, :], t_m, T.sem.arr1, T.sem.ard1),
-                                       (T.land[:, own, 1:4, :], rest, T.sem.arr2, T.sem.ard2)):
-        after(g, "g", deps)
+    deps = ([t_m], [t_m2[0], t_s[0], t_c[0]], [t_m2[1], t_s[1], t_c[1]])
+    for i, piece in enumerate(_pieces(T, own)):
+        after(g, "g", deps[i])
         if relay:
-            sent += _send(g, core, T, topo, piece, helpers, _chip_mask(core, direct, relay, topo), s_far)
+            sent += _send(g, core, T, topo, piece, helpers, _chip_mask(core, direct, relay, topo), far[i])
         if direct:
-            sent += _send(g, core, T, topo, piece, direct, topo.mask(core, direct[0]), s_near)
+            sent += _send(g, core, T, topo, piece, direct, topo.mask(core, direct[0]), near[i])
     n_d, n_x = 0, 0
-    early, late = [own], []
     for p in T.cores:
         if p == core:
             continue
         dp, rp = _plan(p, T, topo)
         if core in dp:
             n_d += _bits(topo.mask(p, core))
-            early.append(slot[p])
         for h, dests in rp:
             if core in dests:
                 n_x += _bits(topo.mask(h, dests[0]))
-                late.append(slot[p])
-    t_d1, t_d2 = [(-1, T.sem.ard1, n_d)], [(-2, T.sem.ard2, n_d)]
-    t_x1, t_x2 = [(-3, T.sem.arr1, n_x)], [(-4, T.sem.arr2, n_x)]
+    here = []
+    for i in range(3):
+        tk = []
+        if n_d:
+            tk.append((-1 - i, near[i], n_d))
+        if n_x:
+            tk.append((-11 - i, far[i], n_x))
+        here.append(tk)
 
-    pool = [T.w0, T.w1, T.w2, T.w3, T.w4, T.w5]
-
-    def rsum(slots, deps):
-        s0, n = min(slots), len(slots)
-        after(V, "v", deps)
-        if n == 4:
-            w = pool.pop()
-            t = done(V.tensor_tensor(out=w[:], in0=T.land[:, s0:s0 + 2, 1:4, :],
-                                     in1=T.land[:, s0 + 2:s0 + 4, 1:4, :], op=ALU.add))
-            parts = [w[:, 0, :, :], w[:, 1, :, :]]
-            after(V, "v", [t])
-        else:
-            parts = [T.land[:, s0 + i, 1:4, :] for i in range(n)]
-        acc, tok, w = parts[0], [], None
-        for p in parts[1:]:
-            w = pool.pop()
-            after(V, "v", tok)
-            tok = [done(V.tensor_tensor(out=w[:, 0, :, :], in0=acc, in1=p, op=ALU.add))]
-            acc = w[:, 0, :, :]
-        return w, tok
-
-    after(V, "v", t_m2)
-    t_a6 = done(V.tensor_scalar(out=T.a6[:], in0=T.land[:, own, 2, :], scalar1=6 * EPS, scalar2=None, op0=ALU.add))
-    after(V, "v", [t_a6])
-    t = done(V.reciprocal(T.ia6[:], T.a6[:]))
-    after(A, "a", [t])
-    t_y0 = done(A.activation(T.y0[:], T.ia6[:], ACT.Sqrt, scale=6.0))
-    after(V, "v", [t_y0])
-    t = done(V.tensor_tensor(out=T.y2[:], in0=T.y0[:], in1=T.y0[:], op=ALU.mult))
-    after(V, "v", [t])
-    t = done(V.tensor_tensor(out=T.ye[:], in0=T.y2[:], in1=T.a6[:], op=ALU.mult))
-    after(V, "v", [t])
-    t = done(V.tensor_scalar(out=T.yf[:], in0=T.ye[:], scalar1=-1.0 / 12, scalar2=1.5, op0=ALU.mult, op1=ALU.add))
-    after(V, "v", [t])
-    t = done(V.tensor_tensor(out=T.rsa[:], in0=T.y0[:], in1=T.yf[:], op=ALU.mult))
-    after(V, "v", [t, t_id])
-    t_ida = [done(V.tensor_scalar(out=T.ida[:, H[h]], in0=T.ident[:], scalar1=col(T.rsa, h), scalar2=None,
-                                  op0=ALU.mult)) for h in (0, 1)]
-
-    after(A, "a", t_d1 + t_x1 + t_m)
-    t_nmu = [done(A.activation(T.jq[:, h, 0:NR], T.land[:, :, 0, h], ACT.Copy, scale=-1.0 / NR,
+    after(A, "a", here[0] + [t_m])
+    t_nmu = [done(A.activation(T.jq[:, h, 0:NR], T.landm[:, :, h], ACT.Copy, scale=-1.0 / NR,
                                accum_out=col(T.nmu, h))) for h in (0, 1)]
     after(A, "a", t_nmu)
-    t_q = [done(A.activation(T.jq[:, 2 + h, 0:NR], T.land[:, :, 0, h], ACT.Square, bias=col(T.nmu, h),
-                             accum_out=col(T.sdd, h))) for h in (0, 1)]
-    after(A, "a", t_tx)
-    t_xm = [done(A.activation(T.xm[:, H[h]], px[h], ACT.Identity, bias=col(T.nmu, h))) for h in (0, 1)]
-    t_nms = [done(A.activation(T.jq[:, 4 + h, 0:NR], T.land[:, :, 0, h], ACT.Copy, scale=-1.0,
-                               accum_out=col(T.nms, h))) for h in (0, 1)]
-
-    we, t_e = rsum(early, t_d2 + rest)
-    after(V, "v", t_e)
-    t = done(V.tensor_scalar(out=we[:, 0, 1, :], in0=we[:, 0, 1, :], scalar1=6 * EPS, scalar2=None, op0=ALU.add))
-    after(V, "v", [t] + t_q)
-    t_e2 = done(V.tensor_tensor(out=we[:, 0, 1, :], in0=we[:, 0, 1, :], in1=T.sdd[:], op=ALU.add))
-    wl, t_l = rsum(late, t_x2)
-    after(V, "v", t_l + [t_e2])
-    t_tot = done(V.tensor_tensor(out=T.tot[:], in0=wl[:, 0, :, :], in1=we[:, 0, :, :], op=ALU.add))
-    after(V, "v", [t_tot])
-    t_iv = done(V.reciprocal(T.iv6[:], T.tot[:, 1, :]))
-
-    t_dg, t_v = [], []
+    t_q = [done(A.activation(T.jq[:, 2 + h, 0:NR], T.landm[:, :, h], ACT.Square, bias=col(T.nmu, h),
+                             accum_out=T.land[:, E1, 3 * h + 1:3 * h + 2])) for h in (0, 1)]
+    t_xm, t_nms = [], []
     for h in (0, 1):
-        after(A, "a", [t_tot, t_nms[h]])
-        t_ct = done(A.activation(col(T.ct, h), T.tot[:, 0, h:h + 1], ACT.Identity, bias=T.tot[:, 2, h:h + 1],
-                                 scale=col(T.nms, h)))
-        after(A, "a", [t_s[h]])
-        t_da = done(A.activation(pd[h], pd[h], ACT.Identity, bias=T.tot[:, 0, h:h + 1]))
-        after(A, "a", [t_iv, t_a6])
-        t = done(A.activation(col(T.r1, h), col(T.iv6, h), ACT.Sqrt, scale=col(T.a6, h)))
-        after(A, "a", [t, t_ida[h]])
-        t_dg.append(done(A.activation(T.dg[:, H[h]], T.ida[:, H[h]], ACT.Copy, scale=col(T.r1, h))))
-        after(V, "v", [t_iv, t_ct, t_xm[h]])
-        t = done(V.tensor_scalar(out=T.uu[:, H[h]], in0=T.xm[:, H[h]], scalar1=col(T.iv6, h), scalar2=col(T.ct, h),
-                                 op0=ALU.mult, op1=ALU.mult))
-        after(V, "v", [t, t_da])
-        t_v.append(done(V.tensor_tensor(out=T.vv[:, H[h]], in0=T.uu[:, H[h]], in1=pd[h], op=ALU.add)))
+        t_xm.append(done(A.activation(T.xm[:, H[h]], T.xts[:, H[h]], ACT.Identity, scale=-128.0, bias=col(T.nmu, h))))
+        t_nms.append(done(A.activation(T.jq[:, 4 + h, 0:NR], T.landm[:, :, h], ACT.Copy, scale=-1.0,
+                                       accum_out=col(T.nms, h))))
+
+    tk = {}
+
+    def v_v6(h):
+        after(V, "v", here[1 + h] + [t_m2[h], t_q[h], t_eps[h]])
+        tk["v6", h] = done(V.tensor_reduce(out=col(T.v6, h), in_=T.land[:, :, 3 * h + 1], axis=AxisListType.X, op=ALU.add))
+
+    def v_iv(h):
+        after(V, "v", [tk["v6", h]])
+        tk["iv", h] = done(V.reciprocal(col(T.iv6, h), col(T.v6, h)))
+
+    def v_uu(h):
+        after(V, "v", [tk["iv", h], tk["ct", h], t_xm[h]])
+        tk["uu", h] = done(V.tensor_scalar(out=T.uu[:, H[h]], in0=T.xm[:, H[h]], scalar1=col(T.iv6, h), scalar2=col(T.ct, h),
+                                           op0=ALU.mult, op1=ALU.mult))
+
+    def v_vv(h):
+        after(V, "v", [tk["uu", h], tk["da", h]])
+        tk["vv", h] = done(V.tensor_tensor(out=T.vv[:, H[h]], in0=T.uu[:, H[h]], in1=pd[h], op=ALU.add))
+
+    def a_sums(h):
+        after(A, "a", here[1 + h] + [t_s[h], t_c[h]])
+        tk["na", h] = done(A.activation(T.jq[:, 6 + h, 0:NR], T.land[:, 0:NR, 3 * h], ACT.Copy, accum_out=col(T.na, h)))
+        tk["sc", h] = done(A.activation(T.jq[:, 8 + h, 0:NR], T.land[:, 0:NR, 3 * h + 2], ACT.Copy, accum_out=col(T.sc, h)))
+
+    def a_ct(h):
+        after(A, "a", [tk["na", h], tk["sc", h], t_nms[h]])
+        tk["ct", h] = done(A.activation(col(T.ct, h), col(T.na, h), ACT.Identity, bias=col(T.sc, h), scale=col(T.nms, h)))
+
+    def a_da(h):
+        after(A, "a", [tk["na", h], t_s[h]])
+        tk["da", h] = done(A.activation(pd[h], pd[h], ACT.Identity, bias=col(T.na, h)))
+
+    def a_r1(h):
+        after(A, "a", [tk["iv", h]])
+        tk["r1", h] = done(A.activation(col(T.r1, h), col(T.iv6, h), ACT.Sqrt))
+
+    def a_dg(h):
+        after(A, "a", [tk["r1", h], t_ida])
+        tk["dg", h] = done(A.activation(T.dg[:, H[h]], T.ida[:], ACT.Copy, scale=col(T.r1, h)))
+
+    v_v6(0)
+    v_iv(0)
+    a_sums(0)
+    a_ct(0)
+    a_da(0)
+    v_v6(1)
+    a_sums(1)
+    v_uu(0)
+    a_r1(0)
+    v_iv(1)
+    a_ct(1)
+    a_dg(0)
+    v_vv(0)
+    a_da(1)
+    v_uu(1)
+    a_r1(1)
+    v_vv(1)
+    a_dg(1)
 
     pieces = ((0, slice(0, 128), T.po0[:, 0:128]), (1, slice(128, 192), T.po1[:, 0:64]), (1, slice(192, 256), T.po2[:, 0:64]))
     t_mm = []
     for h, cs, po in pieces:
-        after(P, "p", [t_v[h], t_dg[h]])
+        after(P, "p", [tk["vv", h], tk["dg", h]])
         t_mm.append(done(P.matmul(po, T.vv[:, H[h]], T.dg[:, cs], True, True)))
     ist, sst = sem()
     for i in (0, 1):
@@ -318,4 +305,7 @@ def rank_program(g, core, T, topo):
     A.dma_start(T.dx[:, cs], T.outs[:, cs]).then_inc(sst, 16)
 
     g.wait_ge(T.sem.sent, sent)
+    for t in made:
+        if t[0] not in waited:
+            after(g, "g", [t])
     g.wait_ge(sst, 48)

@@ -10,20 +10,17 @@ NSEM = 90
 SCRATCH = {
     "xs": ("sbuf", [128, 256], "float32"),
     "dys": ("sbuf", [128, 256], "float32"),
-    "ones": ("sbuf", [128, 128], "float32"),
+    "pr": ("sbuf", [128, 256], "float32"),
+    "fil": ("sbuf", [128, 128], "float32"),
+    "cm": ("sbuf", [128, 132], "float32"),
     "oc": ("sbuf", [128, 4], "float32"),
     "six": ("sbuf", [128, 4], "float32"),
     "c6": ("sbuf", [128, 4], "float32"),
     "ident": ("sbuf", [128, 128], "float32"),
     "ida": ("sbuf", [128, 128], "float32"),
-    "landm": ("sbuf", [128, NR, 4], "float32"),
     "land": ("sbuf", [128, NR + 2, 8], "float32"),
-    "xts": ("sbuf", [128, 256], "float32"),
-    "pr": ("sbuf", [128, 256], "float32"),
     "j2": ("sbuf", [128, 256], "float32"),
-    "j3": ("sbuf", [128, 256], "float32"),
     "jq": ("sbuf", [128, 12, 8], "float32"),
-    "nb": ("sbuf", [128, 2], "float32"),
     "nmu": ("sbuf", [128, 2], "float32"),
     "nms": ("sbuf", [128, 2], "float32"),
     "xm": ("sbuf", [128, 256], "float32"),
@@ -46,7 +43,7 @@ SCRATCH = {
     "po2": ("psum", [128, 512], "float32"),
     "pm": ("psum", [128, 512], "float32"),
 }
-SEMAPHORES = ["arr1", "arr2", "arr3", "ard1", "ard2", "ard3", "sent"] + ["s%d" % i for i in range(NSEM)]
+SEMAPHORES = ["arr1", "arr2", "arr3", "ard1", "ard2", "ard3", "sent", "idn"] + ["s%d" % i for i in range(NSEM)]
 
 
 def _bits(mask):
@@ -86,7 +83,7 @@ def _send(g, core, T, topo, piece, dests, mask, rsem):
 
 
 def _pieces(T, k):
-    return (T.landm[:, k, 0:2], T.land[:, k, 0:3], T.land[:, k, 3:6])
+    return (T.land[:, k, 0:1], T.land[:, k, 1:6], T.land[:, k, 6:8])
 
 
 def rank_program(g, core, T, topo):
@@ -96,13 +93,20 @@ def rank_program(g, core, T, topo):
     if rank is None:
         for c in T.cores:
             direct, relay = _plan(c, T, topo)
-            for h, dests in relay:
+            for j, (h, dests) in enumerate(relay):
                 if h == core:
                     n_in = _bits(_chip_mask(c, direct, relay, topo))
-                    n = 0
-                    for piece, s in zip(_pieces(T, T.rank_of(c)), far):
-                        g.wait_ge(s, n_in)
-                        n += _send(g, core, T, topo, piece, dests, topo.mask(core, dests[0]), s)
+                    mask = topo.mask(core, dests[0])
+                    w = 128 // len(relay)
+                    g.vector.memset(T.fil[:, 0:w], 1.0).then_inc(T.sem.s0, 1)
+                    g.wait_ge(T.sem.s0, 1)
+                    g.affine_select(T.ident[:, j * w:(j + 1) * w], T.fil[:, 0:w], [[-1, w]], AluOpType.is_equal, 0.0,
+                                    -j * w, 1).then_inc(T.sem.s1, 1)
+                    g.wait_ge(T.sem.s1, 1)
+                    n = _send(g, core, T, topo, T.ident[:, j * w:(j + 1) * w], [c], mask & topo.mask(core, c), T.sem.idn)
+                    for piece, sm in zip(_pieces(T, T.rank_of(c)), far):
+                        g.wait_ge(sm, n_in)
+                        n += _send(g, core, T, topo, piece, dests, mask, sm)
                     g.wait_ge(T.sem.sent, n)
         return
 
@@ -136,60 +140,84 @@ def rank_program(g, core, T, topo):
     def col(t, h):
         return t[:, h:h + 1]
 
-    def st(k, h):
-        return T.land[:, own, 3 * h + k:3 * h + k + 1]
-
     H = (slice(0, 128), slice(128, 256))
     px = (T.px0[:, 0:128], T.px1[:, 0:128])
     pd = (T.pd0[:, 0:128], T.pd1[:, 0:128])
+    pdb = (T.pd0, T.pd1)
 
-    Q = (g.sync, A)
-    t_x = [done(Q[h].dma_start(T.xs[:, H[h]], T.x[:, H[h]]), 16) for h in (0, 1)]
-    t_dy = [done(Q[h].dma_start(T.dys[:, H[h]], T.dy[:, H[h]]), 16) for h in (0, 1)]
+    def i_m2(h):
+        return 3 - h
 
+    def i_s(h):
+        return 4 + 2 * h
+
+    def load(dst, src, h):
+        i, s = sem()
+        g.sync.dma_start(dst[0:64, H[h]], src[0:64, H[h]]).then_inc(s, 16)
+        A.dma_start(dst[64:128, H[h]], src[64:128, H[h]]).then_inc(s, 16)
+        made.append((i, s, 32))
+        return (i, s, 32)
+
+    t_x = [load(T.xs, T.x, h) for h in (0, 1)]
+    t_dy = [load(T.dys, T.dy, h) for h in (0, 1)]
+
+    t_fil = done(V.memset(T.fil[:], 1.0 - 1.0 / 128))
     t_six = done(V.memset(T.six[:], 6.0))
-    t_oc = done(V.memset(T.oc[:], 1.0 / 128))
-    t_ones = done(V.memset(T.ones[:], 1.0))
-    t_eps = [done(V.memset(T.land[:, E2, 3 * h + 1:3 * h + 2], 6 * EPS)) for h in (0, 1)]
-    after(g, "g", [t_ones])
-    t_id = done(g.affine_select(T.ident[:], T.ones[:], [[-1, 128]], ALU.is_equal, 0.0, 0, 1))
+    t_oc0 = done(V.memset(T.oc[:, 0:1], 1.0 / 128))
+    t_cmc = done(V.memset(T.cm[:, 128:129], 1.0 / 128))
+    t_oc1 = done(V.memset(T.oc[:, 1:2], -1.0 / (128 * NR)))
+    t_oc2 = done(V.memset(T.oc[:, 2:3], -1.0 / 128))
+    t_eps = done(V.memset(T.land[:, E2, 2:4], 6 * EPS))
+    after(g, "g", [t_fil])
+    t_cm = done(g.affine_select(T.cm[:, 0:128], T.fil[:], [[-1, 128]], ALU.is_equal, -1.0 / 128, 0, 1))
+    direct, relay = _plan(core, T, topo)
+    if relay:
+        t_id = (-21, T.sem.idn, sum(_bits(topo.mask(h, d[0]) & topo.mask(h, core)) for h, d in relay))
+    else:
+        after(V, "v", [t_cm])
+        t_id = done(V.tensor_scalar(out=T.ident[:], in0=T.cm[:, 0:128], scalar1=1.0 / 128, scalar2=None, op0=ALU.add))
     after(A, "a", [t_six])
     t_c6 = done(A.activation(T.c6[:], T.six[:], ACT.Sqrt))
-    after(A, "a", [t_c6, t_id])
-    t_ida = done(A.activation(T.ida[:], T.ident[:], ACT.Copy, scale=T.c6[:, 0:1]))
 
-    t_pm = []
+    after(P, "p", [t_oc0, t_x[0]])
+    t_pm = done(P.matmul(T.pm[:, 0:1], T.xs[:, H[0]], T.oc[:, 0:1], True, True))
+    after(P, "p", [t_cm])
+    t_xc = [done(P.matmul(px[0], T.xs[:, H[0]], T.cm[:, 0:128], True, True))]
+    after(P, "p", [t_x[1], t_cmc])
+    t_xc.append(done(P.matmul(T.px1[:, 0:129], T.xs[:, H[1]], T.cm[:, 0:129], True, True)))
+
+    t_m, t_pr = [], []
+    after(V, "v", [t_pm])
+    t_m.append(done(V.tensor_copy(T.land[:, own, 0:1], T.pm[:, 0:1])))
+    after(V, "v", [t_x[0], t_dy[0]])
+    t_pr.append(done(V.tensor_tensor(out=T.pr[:, H[0]], in0=T.dys[:, H[0]], in1=T.xs[:, H[0]], op=ALU.mult)))
+    after(V, "v", [t_xc[1]])
+    t_m.append(done(V.tensor_copy(T.land[:, own, 1:2], T.px1[:, 128:129])))
+    after(V, "v", [t_x[1], t_dy[1]])
+    t_pr.append(done(V.tensor_tensor(out=T.pr[:, H[1]], in0=T.dys[:, H[1]], in1=T.xs[:, H[1]], op=ALU.mult)))
+
+    t_m2 = []
     for h in (0, 1):
-        after(P, "p", [t_oc, t_x[h]])
-        t_pm.append(done(P.matmul(T.pm[:, h:h + 1], T.xs[:, H[h]], T.oc[:, 0:1], True, True)))
-    after(V, "v", t_pm)
-    t_m = done(V.tensor_copy(T.landm[:, own, 0:2], T.pm[:, 0:2]))
-    t_nb = done(V.tensor_scalar(out=T.nb[:], in0=T.pm[:, 0:2], scalar1=-1.0 / math.sqrt(128.0), scalar2=None, op0=ALU.mult))
-    after(P, "p", [t_id])
-    t_tx, t_td = [], []
+        after(A, "a", [t_xc[h], t_m[h]])
+        t_m2.append(done(A.activation(T.j2[:, H[h]], px[h], ACT.Square, scale=1.0 / math.sqrt(128.0),
+                                      accum_out=T.land[:, own, i_m2(h):i_m2(h) + 1])))
+
+    t_sc = []
     for h in (0, 1):
-        t_tx.append(done(P.transpose(px[h], T.xs[:, H[h]], T.ident[:])))
-        after(P, "p", [t_dy[h]])
+        after(P, "p", [t_dy[h], t_oc1])
+        t_s = done(P.matmul(pdb[h][:, 128:129], T.dys[:, H[h]], T.oc[:, 1:2], True, True))
+        after(P, "p", [t_pr[h], t_oc2])
+        t_c = done(P.matmul(pdb[h][:, 129:130], T.pr[:, H[h]], T.oc[:, 2:3], True, True))
+        after(V, "v", [t_s, t_c])
+        t_sc.append(done(V.tensor_copy(T.land[:, own, i_s(h):i_s(h) + 2], pdb[h][:, 128:130])))
+    t_td = []
+    for h in (0, 1):
+        after(P, "p", [t_id, t_sc[h]])
         t_td.append(done(P.transpose(pd[h], T.dys[:, H[h]], T.ident[:])))
 
-    t_xt, t_m2, t_s, t_c = [], [], [], []
-    for h in (0, 1):
-        after(V, "v", [t_tx[h]])
-        t_xt.append(done(V.tensor_scalar(out=T.xts[:, H[h]], in0=px[h], scalar1=-1.0 / 128, scalar2=None, op0=ALU.mult)))
-        after(A, "a", [t_xt[h], t_nb])
-        t_m2.append(done(A.activation(T.j2[:, H[h]], T.xts[:, H[h]], ACT.Square, scale=-math.sqrt(128.0), bias=col(T.nb, h),
-                                      accum_out=st(1, h))))
-        after(V, "v", [t_td[h], t_xt[h]])
-        t_pr = done(V.tensor_tensor(out=T.pr[:, H[h]], in0=pd[h], in1=T.xts[:, H[h]], op=ALU.mult))
-        after(A, "a", [t_pr, t_td[h]])
-        t_s.append(done(A.activation(T.j3[:, H[h]], pd[h], ACT.Copy, scale=-1.0 / (128 * NR), accum_out=st(0, h))))
-        after(V, "v", [t_pr])
-        t_c.append(done(V.tensor_reduce(out=st(2, h), in_=T.pr[:, H[h]], axis=AxisListType.X, op=ALU.add)))
-
-    direct, relay = _plan(core, T, topo)
     helpers = [h for h, d in relay]
     sent = 0
-    deps = ([t_m], [t_m2[0], t_s[0], t_c[0]], [t_m2[1], t_s[1], t_c[1]])
+    deps = ([t_m[0]], [t_m[1], t_m2[0], t_m2[1], t_sc[0]], [t_sc[1]])
     for i, piece in enumerate(_pieces(T, own)):
         after(g, "g", deps[i])
         if relay:
@@ -208,37 +236,49 @@ def rank_program(g, core, T, topo):
                 n_x += _bits(topo.mask(h, dests[0]))
     here = []
     for i in range(3):
-        tk = []
+        tk0 = []
         if n_d:
-            tk.append((-1 - i, near[i], n_d))
+            tk0.append((-1 - i, near[i], n_d))
         if n_x:
-            tk.append((-11 - i, far[i], n_x))
-        here.append(tk)
-
-    after(A, "a", here[0] + [t_m])
-    t_nmu = [done(A.activation(T.jq[:, h, 0:NR], T.landm[:, :, h], ACT.Copy, scale=-1.0 / NR,
-                               accum_out=col(T.nmu, h))) for h in (0, 1)]
-    after(A, "a", t_nmu)
-    t_q = [done(A.activation(T.jq[:, 2 + h, 0:NR], T.landm[:, :, h], ACT.Square, bias=col(T.nmu, h),
-                             accum_out=T.land[:, E1, 3 * h + 1:3 * h + 2])) for h in (0, 1)]
-    t_xm, t_nms = [], []
-    for h in (0, 1):
-        t_xm.append(done(A.activation(T.xm[:, H[h]], T.xts[:, H[h]], ACT.Identity, scale=-128.0, bias=col(T.nmu, h))))
-        t_nms.append(done(A.activation(T.jq[:, 4 + h, 0:NR], T.landm[:, :, h], ACT.Copy, scale=-1.0,
-                                       accum_out=col(T.nms, h))))
+            tk0.append((-11 - i, far[i], n_x))
+        here.append(tk0)
 
     tk = {}
 
+    def a_nmu(h):
+        after(A, "a", here[h] + [t_m[h]])
+        tk["nmu", h] = done(A.activation(T.jq[:, h, 0:NR], T.land[:, 0:NR, h], ACT.Copy, scale=-1.0 / NR,
+                                         accum_out=col(T.nmu, h)))
+
+    def a_q(h):
+        after(A, "a", [tk["nmu", h]])
+        tk["q", h] = done(A.activation(T.jq[:, 2 + h, 0:NR], T.land[:, 0:NR, h], ACT.Square, bias=col(T.nmu, h),
+                                       accum_out=T.land[:, E1, i_m2(h):i_m2(h) + 1]))
+
+    def a_nms(h):
+        after(A, "a", here[h] + [t_m[h]])
+        tk["nms", h] = done(A.activation(T.jq[:, 4 + h, 0:NR], T.land[:, 0:NR, h], ACT.Copy, scale=-1.0,
+                                         accum_out=col(T.nms, h)))
+
+    def a_ida():
+        after(A, "a", [t_c6, t_id])
+        tk["ida"] = done(A.activation(T.ida[:], T.ident[:], ACT.Copy, scale=T.c6[:, 0:1]))
+
+    def v_xm(h):
+        after(V, "v", [tk["nmu", h], t_m2[h], t_m[h]])
+        tk["xm", h] = done(V.tensor_scalar(out=T.xm[:, H[h]], in0=px[h], scalar1=T.land[:, own, h:h + 1],
+                                           scalar2=col(T.nmu, h), op0=ALU.add, op1=ALU.add))
+
     def v_v6(h):
-        after(V, "v", here[1 + h] + [t_m2[h], t_q[h], t_eps[h]])
-        tk["v6", h] = done(V.tensor_reduce(out=col(T.v6, h), in_=T.land[:, :, 3 * h + 1], axis=AxisListType.X, op=ALU.add))
+        after(V, "v", here[1] + [t_m2[h], tk["q", h], t_eps])
+        tk["v6", h] = done(V.tensor_reduce(out=col(T.v6, h), in_=T.land[:, :, i_m2(h)], axis=AxisListType.X, op=ALU.add))
 
     def v_iv(h):
         after(V, "v", [tk["v6", h]])
         tk["iv", h] = done(V.reciprocal(col(T.iv6, h), col(T.v6, h)))
 
     def v_uu(h):
-        after(V, "v", [tk["iv", h], tk["ct", h], t_xm[h]])
+        after(V, "v", [tk["iv", h], tk["ct", h], tk["xm", h]])
         tk["uu", h] = done(V.tensor_scalar(out=T.uu[:, H[h]], in0=T.xm[:, H[h]], scalar1=col(T.iv6, h), scalar2=col(T.ct, h),
                                            op0=ALU.mult, op1=ALU.mult))
 
@@ -246,17 +286,24 @@ def rank_program(g, core, T, topo):
         after(V, "v", [tk["uu", h], tk["da", h]])
         tk["vv", h] = done(V.tensor_tensor(out=T.vv[:, H[h]], in0=T.uu[:, H[h]], in1=pd[h], op=ALU.add))
 
-    def a_sums(h):
-        after(A, "a", here[1 + h] + [t_s[h], t_c[h]])
-        tk["na", h] = done(A.activation(T.jq[:, 6 + h, 0:NR], T.land[:, 0:NR, 3 * h], ACT.Copy, accum_out=col(T.na, h)))
-        tk["sc", h] = done(A.activation(T.jq[:, 8 + h, 0:NR], T.land[:, 0:NR, 3 * h + 2], ACT.Copy, accum_out=col(T.sc, h)))
+    def a_na(h):
+        after(A, "a", here[1 + h] + [t_sc[h]])
+        tk["na", h] = done(A.activation(T.jq[:, 6 + h, 0:NR], T.land[:, 0:NR, i_s(h)], ACT.Copy, accum_out=col(T.na, h)))
+
+    def a_sc(h):
+        after(A, "a", here[1 + h] + [t_sc[h]])
+        tk["sc", h] = done(A.activation(T.jq[:, 8 + h, 0:NR], T.land[:, 0:NR, i_s(h) + 1], ACT.Copy, accum_out=col(T.sc, h)))
+
+    def v_sc(h):
+        after(V, "v", here[1 + h] + [t_sc[h]])
+        tk["sc", h] = done(V.tensor_reduce(out=col(T.sc, h), in_=T.land[:, 0:NR, i_s(h) + 1], axis=AxisListType.X, op=ALU.add))
 
     def a_ct(h):
-        after(A, "a", [tk["na", h], tk["sc", h], t_nms[h]])
+        after(A, "a", [tk["na", h], tk["sc", h], tk["nms", h]])
         tk["ct", h] = done(A.activation(col(T.ct, h), col(T.na, h), ACT.Identity, bias=col(T.sc, h), scale=col(T.nms, h)))
 
     def a_da(h):
-        after(A, "a", [tk["na", h], t_s[h]])
+        after(A, "a", [tk["na", h], t_td[h]])
         tk["da", h] = done(A.activation(pd[h], pd[h], ACT.Identity, bias=col(T.na, h)))
 
     def a_r1(h):
@@ -264,19 +311,30 @@ def rank_program(g, core, T, topo):
         tk["r1", h] = done(A.activation(col(T.r1, h), col(T.iv6, h), ACT.Sqrt))
 
     def a_dg(h):
-        after(A, "a", [tk["r1", h], t_ida])
+        after(A, "a", [tk["r1", h], tk["ida"]])
         tk["dg", h] = done(A.activation(T.dg[:, H[h]], T.ida[:], ACT.Copy, scale=col(T.r1, h)))
 
+    a_nmu(0)
+    a_q(0)
+    a_nms(0)
+    a_ida()
+    v_xm(0)
+    a_nmu(1)
+    a_na(0)
+    a_sc(0)
+    a_q(1)
+    a_ct(0)
+    a_nms(1)
+    a_da(0)
     v_v6(0)
     v_iv(0)
-    a_sums(0)
-    a_ct(0)
-    a_da(0)
+    v_xm(1)
     v_v6(1)
-    a_sums(1)
+    v_iv(1)
+    a_na(1)
+    v_sc(1)
     v_uu(0)
     a_r1(0)
-    v_iv(1)
     a_ct(1)
     a_dg(0)
     v_vv(0)

import math
from concourse.bass import DstId, RemoteDMATransfer
from concourse.mybir import AluOpType, AxisListType, ActivationFunctionType

NSIM = 256
NR = 6
EPS = 0.01
NSEM = 90

SCRATCH = {
    "xs": ("sbuf", [128, 256], "float32"),
    "dys": ("sbuf", [128, 256], "float32"),
    "pr": ("sbuf", [128, 256], "float32"),
    "fil": ("sbuf", [128, 128], "float32"),
    "cm": ("sbuf", [128, 132], "float32"),
    "oc": ("sbuf", [128, 4], "float32"),
    "six": ("sbuf", [128, 4], "float32"),
    "c6": ("sbuf", [128, 4], "float32"),
    "ident": ("sbuf", [128, 128], "float32"),
    "ida": ("sbuf", [128, 128], "float32"),
    "land": ("sbuf", [128, NR + 2, 8], "float32"),
    "j2": ("sbuf", [128, 256], "float32"),
    "jq": ("sbuf", [128, 12, 8], "float32"),
    "nmu": ("sbuf", [128, 2], "float32"),
    "nms": ("sbuf", [128, 2], "float32"),
    "xm": ("sbuf", [128, 256], "float32"),
    "v6": ("sbuf", [128, 2], "float32"),
    "iv6": ("sbuf", [128, 2], "float32"),
    "na": ("sbuf", [128, 2], "float32"),
    "sc": ("sbuf", [128, 2], "float32"),
    "ct": ("sbuf", [128, 2], "float32"),
    "r1": ("sbuf", [128, 2], "float32"),
    "dg": ("sbuf", [128, 256], "float32"),
    "uu": ("sbuf", [128, 256], "float32"),
    "vv": ("sbuf", [128, 256], "float32"),
    "outs": ("sbuf", [128, 256], "float32"),
    "px0": ("psum", [128, 512], "float32"),
    "px1": ("psum", [128, 512], "float32"),
    "pd0": ("psum", [128, 512], "float32"),
    "pd1": ("psum", [128, 512], "float32"),
    "po0": ("psum", [128, 512], "float32"),
    "po1": ("psum", [128, 512], "float32"),
    "po2": ("psum", [128, 512], "float32"),
    "pm": ("psum", [128, 512], "float32"),
}
SEMAPHORES = ["arr1", "arr2", "arr3", "ard1", "ard2", "ard3", "sent", "idn"] + ["s%d" % i for i in range(NSEM)]


def _bits(mask):
    return bin(mask).count("1")


def _plan(c, T, topo):
    others = [p for p in T.cores if p != c]
    direct = [p for p in others if topo.may_write(c, p)]
    cross = [p for p in others if not topo.may_write(c, p)]
    cand = [k for k in range(NSIM)
            if k != c and T.rank_of(k) is None and topo.host(k) == topo.host(c) and topo.chip(k) == topo.chip(c)
            and all(topo.may_write(k, p) for p in cross)]
    cand.sort(key=lambda k: (topo.die(k) != topo.die(c), k))
    relay = [(cand[i // 2], cross[i:i + 2]) for i in range(0, len(cross), 2)]
    return direct, relay


def _chip_mask(c, direct, relay, topo):
    m = topo.mask(c, relay[0][0])
    for p in direct:
        if m & ~topo.mask(c, p):
            m = m & ~topo.mask(c, p)
    return m


def _send(g, core, T, topo, piece, dests, mask, rsem):
    ids = []
    for d in dests:
        rid, pid = topo.addr(d, core)
        ids.append(DstId(rid=rid, pnc=pid))
    g.remote_dma_fused(
        [RemoteDMATransfer(dst_ids=ids, dma_engine_mask=mask, remote_sem=rsem,
                           srcs=[piece], dsts=[piece for d in dests], alu_op=0)],
        local_sem=T.sem.sent)
    return _bits(mask)


def _pieces(T, k):
    return (T.land[:, k, 0:1], T.land[:, k, 1:6], T.land[:, k, 6:8])


def rank_program(g, core, T, topo):
    rank = T.rank_of(core)
    far = (T.sem.arr1, T.sem.arr2, T.sem.arr3)
    near = (T.sem.ard1, T.sem.ard2, T.sem.ard3)
    if rank is None:
        for c in T.cores:
            direct, relay = _plan(c, T, topo)
            for j, (h, dests) in enumerate(relay):
                if h == core:
                    n_in = _bits(_chip_mask(c, direct, relay, topo))
                    mask = topo.mask(core, dests[0])
                    w = 128 // len(relay)
                    g.vector.memset(T.fil[:, 0:w], 1.0).then_inc(T.sem.s0, 1)
                    g.wait_ge(T.sem.s0, 1)
                    g.affine_select(T.ident[:, j * w:(j + 1) * w], T.fil[:, 0:w], [[-1, w]], AluOpType.is_equal, 0.0,
                                    -j * w, 1).then_inc(T.sem.s1, 1)
                    g.wait_ge(T.sem.s1, 1)
                    n = _send(g, core, T, topo, T.ident[:, j * w:(j + 1) * w], [c], mask & topo.mask(core, c), T.sem.idn)
                    for piece, sm in zip(_pieces(T, T.rank_of(c)), far):
                        g.wait_ge(sm, n_in)
                        n += _send(g, core, T, topo, piece, dests, mask, sm)
                    g.wait_ge(T.sem.sent, n)
        return

    V, A, P = g.vector, g.scalar, g.tensor
    ALU, ACT = AluOpType, ActivationFunctionType
    own = rank
    E1, E2 = NR, NR + 1
    cnt = [0]
    seen = {}
    waited = {}
    made = []

    def sem():
        i = cnt[0]
        cnt[0] += 1
        return i, T.sem["s%d" % i]

    def done(instr, n=1):
        i, s = sem()
        instr.then_inc(s, n)
        made.append((i, s, n))
        return (i, s, n)

    def after(q, qn, toks):
        for (i, s, v) in toks:
            waited[i] = True
            if (qn, i) not in seen:
                seen[(qn, i)] = True
                q.wait_ge(s, v)

    def col(t, h):
        return t[:, h:h + 1]

    H = (slice(0, 128), slice(128, 256))
    px = (T.px0[:, 0:128], T.px1[:, 0:128])
    pd = (T.pd0[:, 0:128], T.pd1[:, 0:128])
    pdb = (T.pd0, T.pd1)

    def i_m2(h):
        return 3 - h

    def i_s(h):
        return 4 + 2 * h

    def load(dst, src, h):
        i, s = sem()
        g.sync.dma_start(dst[0:64, H[h]], src[0:64, H[h]]).then_inc(s, 16)
        A.dma_start(dst[64:128, H[h]], src[64:128, H[h]]).then_inc(s, 16)
        made.append((i, s, 32))
        return (i, s, 32)

    t_x = [load(T.xs, T.x, h) for h in (0, 1)]
    t_dy = [load(T.dys, T.dy, h) for h in (0, 1)]

    t_fil = done(V.memset(T.fil[:], 1.0 - 1.0 / 128))
    t_six = done(V.memset(T.six[:], 6.0))
    t_oc0 = done(V.memset(T.oc[:, 0:1], 1.0 / 128))
    t_cmc = done(V.memset(T.cm[:, 128:129], 1.0 / 128))
    t_oc1 = done(V.memset(T.oc[:, 1:2], -1.0 / (128 * NR)))
    t_oc2 = done(V.memset(T.oc[:, 2:3], -1.0 / 128))
    t_eps = done(V.memset(T.land[:, E2, 2:4], 6 * EPS))
    after(g, "g", [t_fil])
    t_cm = done(g.affine_select(T.cm[:, 0:128], T.fil[:], [[-1, 128]], ALU.is_equal, -1.0 / 128, 0, 1))
    direct, relay = _plan(core, T, topo)
    if relay:
        t_id = (-21, T.sem.idn, sum(_bits(topo.mask(h, d[0]) & topo.mask(h, core)) for h, d in relay))
    else:
        after(V, "v", [t_cm])
        t_id = done(V.tensor_scalar(out=T.ident[:], in0=T.cm[:, 0:128], scalar1=1.0 / 128, scalar2=None, op0=ALU.add))
    after(A, "a", [t_six])
    t_c6 = done(A.activation(T.c6[:], T.six[:], ACT.Sqrt))

    after(P, "p", [t_oc0, t_x[0]])
    t_pm = done(P.matmul(T.pm[:, 0:1], T.xs[:, H[0]], T.oc[:, 0:1], True, True))
    after(P, "p", [t_cm])
    t_xc = [done(P.matmul(px[0], T.xs[:, H[0]], T.cm[:, 0:128], True, True))]
    after(P, "p", [t_x[1], t_cmc])
    t_xc.append(done(P.matmul(T.px1[:, 0:129], T.xs[:, H[1]], T.cm[:, 0:129], True, True)))

    t_m, t_pr = [], []
    after(V, "v", [t_pm])
    t_m.append(done(V.tensor_copy(T.land[:, own, 0:1], T.pm[:, 0:1])))
    after(V, "v", [t_x[0], t_dy[0]])
    t_pr.append(done(V.tensor_tensor(out=T.pr[:, H[0]], in0=T.dys[:, H[0]], in1=T.xs[:, H[0]], op=ALU.mult)))
    after(V, "v", [t_xc[1]])
    t_m.append(done(V.tensor_copy(T.land[:, own, 1:2], T.px1[:, 128:129])))
    after(V, "v", [t_x[1], t_dy[1]])
    t_pr.append(done(V.tensor_tensor(out=T.pr[:, H[1]], in0=T.dys[:, H[1]], in1=T.xs[:, H[1]], op=ALU.mult)))

    t_m2 = []
    for h in (0, 1):
        after(A, "a", [t_xc[h], t_m[h]])
        t_m2.append(done(A.activation(T.j2[:, H[h]], px[h], ACT.Square, scale=1.0 / math.sqrt(128.0),
                                      accum_out=T.land[:, own, i_m2(h):i_m2(h) + 1])))

    t_sc = []
    for h in (0, 1):
        after(P, "p", [t_dy[h], t_oc1])
        t_s = done(P.matmul(pdb[h][:, 128:129], T.dys[:, H[h]], T.oc[:, 1:2], True, True))
        after(P, "p", [t_pr[h], t_oc2])
        t_c = done(P.matmul(pdb[h][:, 129:130], T.pr[:, H[h]], T.oc[:, 2:3], True, True))
        after(V, "v", [t_s, t_c])
        t_sc.append(done(V.tensor_copy(T.land[:, own, i_s(h):i_s(h) + 2], pdb[h][:, 128:130])))
    t_td = []
    for h in (0, 1):
        after(P, "p", [t_id, t_sc[h]])
        t_td.append(done(P.transpose(pd[h], T.dys[:, H[h]], T.ident[:])))

    helpers = [h for h, d in relay]
    sent = 0
    deps = ([t_m[0]], [t_m[1], t_m2[0], t_m2[1], t_sc[0]], [t_sc[1]])
    for i, piece in enumerate(_pieces(T, own)):
        after(g, "g", deps[i])
        if relay:
            sent += _send(g, core, T, topo, piece, helpers, _chip_mask(core, direct, relay, topo), far[i])
        if direct:
            sent += _send(g, core, T, topo, piece, direct, topo.mask(core, direct[0]), near[i])
    n_d, n_x = 0, 0
    for p in T.cores:
        if p == core:
            continue
        dp, rp = _plan(p, T, topo)
        if core in dp:
            n_d += _bits(topo.mask(p, core))
        for h, dests in rp:
            if core in dests:
                n_x += _bits(topo.mask(h, dests[0]))
    here = []
    for i in range(3):
        tk0 = []
        if n_d:
            tk0.append((-1 - i, near[i], n_d))
        if n_x:
            tk0.append((-11 - i, far[i], n_x))
        here.append(tk0)

    tk = {}

    def a_nmu(h):
        after(A, "a", here[h] + [t_m[h]])
        tk["nmu", h] = done(A.activation(T.jq[:, h, 0:NR], T.land[:, 0:NR, h], ACT.Copy, scale=-1.0 / NR,
                                         accum_out=col(T.nmu, h)))

    def a_q(h):
        after(A, "a", [tk["nmu", h]])
        tk["q", h] = done(A.activation(T.jq[:, 2 + h, 0:NR], T.land[:, 0:NR, h], ACT.Square, bias=col(T.nmu, h),
                                       accum_out=T.land[:, E1, i_m2(h):i_m2(h) + 1]))

    def a_nms(h):
        after(A, "a", here[h] + [t_m[h]])
        tk["nms", h] = done(A.activation(T.jq[:, 4 + h, 0:NR], T.land[:, 0:NR, h], ACT.Copy, scale=-1.0,
                                         accum_out=col(T.nms, h)))

    def a_ida():
        after(A, "a", [t_c6, t_id])
        tk["ida"] = done(A.activation(T.ida[:], T.ident[:], ACT.Copy, scale=T.c6[:, 0:1]))

    def v_xm(h):
        after(V, "v", [tk["nmu", h], t_m2[h], t_m[h]])
        tk["xm", h] = done(V.tensor_scalar(out=T.xm[:, H[h]], in0=px[h], scalar1=T.land[:, own, h:h + 1],
                                           scalar2=col(T.nmu, h), op0=ALU.add, op1=ALU.add))

    def v_v6(h):
        after(V, "v", here[1] + [t_m2[h], tk["q", h], t_eps])
        tk["v6", h] = done(V.tensor_reduce(out=col(T.v6, h), in_=T.land[:, :, i_m2(h)], axis=AxisListType.X, op=ALU.add))

    def v_iv(h):
        after(V, "v", [tk["v6", h]])
        tk["iv", h] = done(V.reciprocal(col(T.iv6, h), col(T.v6, h)))

    def v_uu(h):
        after(V, "v", [tk["iv", h], tk["ct", h], tk["xm", h]])
        tk["uu", h] = done(V.tensor_scalar(out=T.uu[:, H[h]], in0=T.xm[:, H[h]], scalar1=col(T.iv6, h), scalar2=col(T.ct, h),
                                           op0=ALU.mult, op1=ALU.mult))

    def v_vv(h):
        after(V, "v", [tk["uu", h], tk["da", h]])
        tk["vv", h] = done(V.tensor_tensor(out=T.vv[:, H[h]], in0=T.uu[:, H[h]], in1=pd[h], op=ALU.add))

    def a_na(h):
        after(A, "a", here[1 + h] + [t_sc[h]])
        tk["na", h] = done(A.activation(T.jq[:, 6 + h, 0:NR], T.land[:, 0:NR, i_s(h)], ACT.Copy, accum_out=col(T.na, h)))

    def a_sc(h):
        after(A, "a", here[1 + h] + [t_sc[h]])
        tk["sc", h] = done(A.activation(T.jq[:, 8 + h, 0:NR], T.land[:, 0:NR, i_s(h) + 1], ACT.Copy, accum_out=col(T.sc, h)))

    def v_sc(h):
        after(V, "v", here[1 + h] + [t_sc[h]])
        tk["sc", h] = done(V.tensor_reduce(out=col(T.sc, h), in_=T.land[:, 0:NR, i_s(h) + 1], axis=AxisListType.X, op=ALU.add))

    def a_ct(h):
        after(A, "a", [tk["na", h], tk["sc", h], tk["nms", h]])
        tk["ct", h] = done(A.activation(col(T.ct, h), col(T.na, h), ACT.Identity, bias=col(T.sc, h), scale=col(T.nms, h)))

    def a_da(h):
        after(A, "a", [tk["na", h], t_td[h]])
        tk["da", h] = done(A.activation(pd[h], pd[h], ACT.Identity, bias=col(T.na, h)))

    def a_r1(h):
        after(A, "a", [tk["iv", h]])
        tk["r1", h] = done(A.activation(col(T.r1, h), col(T.iv6, h), ACT.Sqrt))

    def a_dg(h):
        after(A, "a", [tk["r1", h], tk["ida"]])
        tk["dg", h] = done(A.activation(T.dg[:, H[h]], T.ida[:], ACT.Copy, scale=col(T.r1, h)))

    a_nmu(0)
    a_q(0)
    a_nms(0)
    a_ida()
    v_xm(0)
    a_nmu(1)
    a_na(0)
    a_sc(0)
    a_q(1)
    a_ct(0)
    a_nms(1)
    a_da(0)
    v_v6(0)
    v_iv(0)
    v_xm(1)
    v_v6(1)
    v_iv(1)
    a_na(1)
    v_sc(1)
    v_uu(0)
    a_r1(0)
    a_ct(1)
    a_dg(0)
    v_vv(0)
    a_da(1)
    v_uu(1)
    a_r1(1)
    v_vv(1)
    a_dg(1)

    pieces = ((0, slice(0, 128), T.po0[:, 0:128]), (1, slice(128, 192), T.po1[:, 0:64]), (1, slice(192, 256), T.po2[:, 0:64]))
    t_mm = []
    for h, cs, po in pieces:
        after(P, "p", [tk["vv", h], tk["dg", h]])
        t_mm.append(done(P.matmul(po, T.vv[:, H[h]], T.dg[:, cs], True, True)))
    ist, sst = sem()
    for i in (0, 1):
        h, cs, po = pieces[i]
        after(V, "v", [t_mm[i]])
        t_cp = done(V.tensor_copy(T.outs[:, cs], po))
        after(g.sync, "s", [t_cp])
        g.sync.dma_start(T.dx[:, cs], T.outs[:, cs]).then_inc(sst, 16)
    h, cs, po = pieces[2]
    after(A, "a", [t_mm[2]])
    t_cp = done(A.activation(T.outs[:, cs], po, ACT.Copy))
    after(A, "a", [t_cp])
    A.dma_start(T.dx[:, cs], T.outs[:, cs]).then_inc(sst, 16)

    g.wait_ge(T.sem.sent, sent)
    for t in made:
        if t[0] not in waited:
            after(g, "g", [t])
    g.wait_ge(sst, 48)
